import numpy as np
import ml_dtypes


def mxq(x, axis, fmt="e4m3"):
    dtype, down = {"e4m3": (ml_dtypes.float8_e4m3fn, 7), "e5m2": (ml_dtypes.float8_e5m2, 14)}[fmt]
    v = np.moveaxis(np.asarray(x, np.float32).astype(ml_dtypes.bfloat16).astype(np.float64), axis, -1)
    blocks = v.reshape(v.shape[:-1] + (-1, 32))
    amax = np.abs(blocks).max(-1, keepdims=True)
    byte = np.maximum(np.where(amax > 0, np.frexp(amax)[1] - 1 + 127, 0) - down, 1)
    scale = np.exp2(byte - 127.0)
    codes = (blocks / scale).astype(np.float32).astype(dtype).astype(np.float64)
    return np.moveaxis((codes * scale).reshape(v.shape), -1, axis)


WIDE = False


def mx_kscale(k):
    if not WIDE:
        return np.ones(k)
    levels = np.array([10, -10, 5, -5, 0])
    if k % 512:
        return np.exp2(np.random.permutation(np.resize(levels, k // 32))).repeat(32)
    a = np.empty((k // 512, 16))
    for p in range(k // 512):
        a[p, :8] = np.random.permutation(np.resize(levels, 8))
        for g in range(8):
            far = levels[np.abs(levels - a[p, g]) >= 10]
            a[p, g + 8] = far[np.random.randint(len(far))]
    return np.exp2(a.ravel()).repeat(32)


def f64(x):
    return np.asarray(x).astype(np.float64)


def striped(idx):
    return np.tile(idx.reshape(-1, 16).T, (8, 1)).astype(np.uint16)


def unstriped(offs):
    return offs[:16].T.reshape(-1).astype(np.int64)


E2M1 = np.array([0.0, 0.5, 1.0, 1.5, 2.0, 3.0, 4.0, 6.0, -0.0, -0.5, -1.0, -1.5, -2.0, -3.0, -4.0, -6.0])


def pack_weight(w, fmt):
    k, n = w.shape
    w = f64(np.asarray(w, np.float32).astype(ml_dtypes.bfloat16)).reshape(k // 32, 32, n)
    amax = np.abs(w).max(1)
    if fmt == "e4m3":
        byte = np.frexp(amax)[1] - 1 + 127 - 7
    else:
        mant, ex = np.frexp(amax / 6.0)
        byte = np.where(mant > 0.5, ex, ex - 1) + 127
    byte = np.clip(np.where(amax > 0, byte, 1), 1, 254)
    scaled = (w * np.exp2(127.0 - byte)[:, None, :]).reshape(k, n).astype(np.float32)
    by_word = np.ascontiguousarray(scaled.reshape(k // 512, 128, 4, n).transpose(0, 1, 3, 2))
    if fmt == "e4m3":
        words = by_word.astype(ml_dtypes.float8_e4m3fn).view(np.uint8)
    else:
        c = by_word.astype(ml_dtypes.float4_e2m1fn).view(np.uint8) & 0xF
        words = (c[..., 0::2] | (c[..., 1::2] << 4)).reshape(k // 512, 128, 2 * n)
    return np.ascontiguousarray(words), np.ascontiguousarray(byte.astype(np.uint8).reshape(k // 512, 16, n))


def unpack_weight(words, scales, fmt):
    g, _, n = scales.shape
    words = np.ascontiguousarray(words).reshape(g, 128, n, -1)
    if fmt == "e4m3":
        vals = words.view(ml_dtypes.float8_e4m3fn).astype(np.float64)
    else:
        nib = np.empty((g, 128, n, 4), np.uint8)
        nib[..., 0::2] = words & 0xF
        nib[..., 1::2] = words >> 4
        vals = E2M1[nib]
    vals = vals * np.repeat(np.exp2(scales.astype(np.float64) - 127.0), 8, axis=1)[..., None]
    return vals.transpose(0, 1, 3, 2).reshape(g * 512, n)


def gelu(v):
    return 0.5 * v * (1.0 + np.tanh(np.sqrt(2.0 / np.pi) * (v + 0.044715 * v**3)))


K, K2, H, N, T, T2, S = 1024, 512, 512, 384, 4096, 2048, 1024

def setup_inputs():
    n = np.random.standard_normal
    s, s2, u = mx_kscale(K)[:, None], mx_kscale(K2)[:, None], mx_kscale(H)[:, None]
    tab_words, tab_scales = pack_weight(n((K, T)) * s, "e4m3")
    tab2_words, tab2_scales = pack_weight(n((K2, T2)) * s2, "e4m3")
    wbr_words, wbr_scales = pack_weight(n((K2, H)) / s2 / np.sqrt(K2), "e2m1")
    wbi_words, wbi_scales = pack_weight(n((K2, H)) / s2 / np.sqrt(K2), "e2m1")
    beam_words, beam_scales = pack_weight(n((H, N)) / u / np.sqrt(H), "e4m3")
    return {
        "tab_words": tab_words, "tab_scales": tab_scales,
        "tab2_words": tab2_words, "tab2_scales": tab2_scales,
        "offs": striped(np.random.permutation(T)[:S]),
        "offs2": striped(np.random.permutation(T2)[:S]),
        "war": (n((K, H)) / s * u.T / np.sqrt(K)).astype(np.float32),
        "wai": (n((K, H)) / s * u.T / np.sqrt(K)).astype(np.float32),
        "wbr_words": wbr_words, "wbr_scales": wbr_scales,
        "wbi_words": wbi_words, "wbi_scales": wbi_scales,
        "beam_words": beam_words, "beam_scales": beam_scales,
        "gain": np.exp(0.3 * n(N)).astype(np.float32),
        "base": (0.5 * n(N)).astype(np.float32),
    }

def reference(tab_words, tab_scales, tab2_words, tab2_scales, offs, offs2, war, wai,
              wbr_words, wbr_scales, wbi_words, wbi_scales, beam_words, beam_scales, gain, base):
    v = unpack_weight(tab_words, tab_scales, "e4m3")[:, unstriped(offs)]
    v2 = unpack_weight(tab2_words, tab2_scales, "e4m3")[:, unstriped(offs2)]
    ar = mxq(f64(war), 0, "e4m3").T @ v
    ai = mxq(f64(wai), 0, "e4m3").T @ v
    br = unpack_weight(wbr_words, wbr_scales, "e2m1").T @ v2
    bi = unpack_weight(wbi_words, wbi_scales, "e2m1").T @ v2
    h = ar * br + ai * bi
    y = unpack_weight(beam_words, beam_scales, "e4m3").T @ mxq(h, 0, "e4m3")
    return f64(gain)[:, None] * y + f64(base)[:, None]

@@ -1,0 +1,249 @@
+from contextlib import ExitStack
+
+import concourse.mybir as mybir
+from concourse.masks import make_identity
+
+K, K2, H, N, T, T2, S = 1024, 512, 512, 384, 4096, 2048, 1024
+FLOPS = 2 * S * (2 * K * H + 2 * K2 * H + H * N)
+
+F32 = mybir.dt.float32
+BF16 = mybir.dt.bfloat16
+I32 = mybir.dt.int32
+U32 = mybir.dt.uint32
+U16 = mybir.dt.uint16
+U8 = mybir.dt.uint8
+FP8X4 = mybir.dt.float8_e4m3fn_x4
+FP4X4 = mybir.dt.float4_e2m1fn_x4
+MULT = mybir.AluOpType.mult
+ADD = mybir.AluOpType.add
+IDENTITY = mybir.ActivationFunctionType.Identity
+
+P = 128
+PACK = 4
+K_PASS = P * PACK
+PASSES = K // K_PASS
+TOK = 128
+TILES = S // TOK
+PAIR = 2 * TOK
+PAIRS = S // PAIR
+HALF = H // 2
+BEAM_TILES = N // P
+SCALE_ROW = (4, 8)
+
+
+def tile_list_reference_matched_beams_kernel(
+    tc, tab_words, tab_scales, tab2_words, tab2_scales, offs, offs2, war, wai,
+    wbr_words, wbr_scales, wbi_words, wbi_scales, beam_words, beam_scales, gain, base, out,
+):
+    nc = tc.nc
+    with ExitStack() as ctx:
+        lists = ctx.enter_context(tc.tile_pool(name="lists", bufs=1))
+        keep = ctx.enter_context(tc.tile_pool(name="keep", bufs=1))
+        psum = ctx.enter_context(tc.psum_pool(name="psum", bufs=1))
+
+        def sbuf(name, shape, dtype):
+            return keep.tile(shape, dtype, name=name, align_bytes=64)
+
+        idx = lists.tile([P, S // 16], U16, name="idx")
+        idx2 = lists.tile([P, S // 16], U16, name="idx2")
+
+        v_words = [sbuf(f"v_words{a}", [P, T], I32) for a in range(PASSES)]
+        v_scales = sbuf("v_scales", [P, T // 4], I32)
+        v2_words = sbuf("v2_words", [P, T2], I32)
+        v2_scales = sbuf("v2_scales", [P, T2 // 4], I32)
+        wb_words = [sbuf(f"wb_words{m}", [P, 2 * H // 4], I32) for m in range(2)]
+        wb_scales = [sbuf(f"wb_scales{m}", [P, H // 4], I32) for m in range(2)]
+        bm_words = sbuf("bm_words", [P, N], I32)
+        bm_scales = sbuf("bm_scales", [P, N // 4], I32)
+        gain_cols = sbuf("gain_cols", [P, BEAM_TILES], F32)
+        base_cols = sbuf("base_cols", [P, BEAM_TILES], F32)
+        ident = sbuf("ident", [P, P], F32)
+
+        nc.vector.memset(v2_scales[:], 0)
+        nc.vector.memset(wb_scales[0][:], 0)
+        nc.vector.memset(v_scales[:], 0)
+        nc.vector.memset(wb_scales[1][:], 0)
+        nc.vector.memset(bm_scales[:], 0)
+
+        def load_scale_rows(queue, plane, rows):
+            for q in range(4):
+                queue.dma_start(out=plane[32 * q : 32 * q + 4, :], in_=rows[0, 4 * q : 4 * q + 4, :].bitcast(I32))
+
+        def words_of(dram, a):
+            return dram[a].rearrange("p t i -> p (t i)").bitcast(I32)
+
+        def load_table_half(a, u):
+            cols = slice(u * T // 2, (u + 1) * T // 2)
+            nc.sync.dma_start(out=v_words[a][:, cols], in_=words_of(tab_words, a)[:, cols])
+
+        nc.sync.dma_start(idx2[:], offs2)
+        nc.sync.dma_start(out=v2_words[:], in_=words_of(tab2_words, 0))
+        load_scale_rows(nc.scalar, v2_scales, tab2_scales)
+        load_scale_rows(nc.scalar, wb_scales[0], wbr_scales)
+        for q in range(4):
+            nc.gpsimd.dma_start(
+                out=v_scales[32 * q + 4 : 32 * q + 12, :],
+                in_=tab_scales[:, 4 * q : 4 * q + 4, :].bitcast(I32),
+            )
+        nc.sync.dma_start(out=wb_words[0][:], in_=wbr_words[0].bitcast(I32))
+        load_table_half(0, 0)
+        nc.sync.dma_start(idx[:], offs)
+        load_table_half(0, 1)
+        nc.sync.dma_start(out=wb_words[1][:], in_=wbi_words[0].bitcast(I32))
+        load_table_half(1, 0)
+        load_scale_rows(nc.sync, wb_scales[1], wbi_scales)
+        load_table_half(1, 1)
+
+        wa_raw = {}
+        for half in range(2):
+            for m, w in enumerate((war, wai)):
+                for a in range(PASSES):
+                    raw = sbuf(f"wa_raw{half}{m}{a}", [P, PACK, HALF], F32)
+                    rows = w[a * K_PASS : (a + 1) * K_PASS, half * HALF : (half + 1) * HALF]
+                    nc.sync.dma_start(out=raw[:], in_=rows.rearrange("(p j) c -> p j c", j=PACK))
+                    wa_raw[half, m, a] = raw
+        nc.sync.dma_start(out=bm_words[:], in_=words_of(beam_words, 0))
+        load_scale_rows(nc.sync, bm_scales, beam_scales)
+        with nc.allow_non_contiguous_dma(reason="one gain and one baseline for each partition"):
+            nc.sync.dma_start(out=gain_cols[:], in_=gain.rearrange("(c p) -> p c", p=P))
+            nc.sync.dma_start(out=base_cols[:], in_=base.rearrange("(c p) -> p c", p=P))
+        make_identity(nc, ident[:])
+
+        def gather(picked, window, offsets, first, last):
+            nc.vector.tensor_copy(picked[:, first:last], window.indirect(offsets[:, first // 16 : last // 16]))
+
+        g_words = [sbuf(f"g_words{a}", [P, S], U32) for a in range(PASSES)]
+        g_scales = sbuf("g_scales", [P, S], U8)
+        g2_words = sbuf("g2_words", [P, S], U32)
+        g2_scales = sbuf("g2_scales", [P, S], U8)
+
+        for first in (0, S // 2):
+            gather(g2_words, v2_words[:].bitcast(U32), idx2, first, first + S // 2)
+            gather(g2_scales, v2_scales[:].bitcast(U8), idx2, first, first + S // 2)
+        gather(g_words[0], v_words[0][:].bitcast(U32), idx, 0, S)
+        gather(g_scales, v_scales[:].bitcast(U8), idx, 0, S)
+        for first in (0, S // 2):
+            gather(g_words[1], v_words[1][:].bitcast(U32), idx, first, first + S // 2)
+
+        b_vals = [sbuf(f"b_vals{m}", [P, TILES, H], F32) for m in range(2)]
+        for m in range(2):
+            for j in range(TILES):
+                tok = slice(j * TOK, (j + 1) * TOK)
+                bank = psum.tile([P, H], F32, name="mm", tag="mm", bufs=4)
+                nc.tensor.matmul_mx(
+                    out=bank[:],
+                    lhsT=g2_words[:, tok].bitcast(FP8X4),
+                    lhsT_scale=g2_scales[:, tok],
+                    rhs=wb_words[m][:].bitcast(U8).bitcast(FP4X4),
+                    rhs_scale=wb_scales[m][:].bitcast(U8),
+                    start=True,
+                    stop=True,
+                )
+                nc.scalar.copy(out=b_vals[m][:, j, :], in_=bank[:])
+
+        def round_weights(copy, half, m):
+            grouped = sbuf(f"wa_bf{half}{m}", [P, PASSES, HALF, PACK], BF16)
+            for a in range(PASSES):
+                copy(
+                    out=grouped[:, a, :, :].rearrange("p (c i) j -> p c j i", i=4),
+                    in_=wa_raw[half, m, a][:].rearrange("p j (c i) -> p c j i", i=4),
+                )
+            return grouped
+
+        def quantize_weights(grouped, half, m):
+            codes = sbuf(f"wa_codes{half}{m}", [P, PASSES, HALF], U32)
+            scales = sbuf(f"wa_scales{half}{m}", [P, PASSES, HALF], U8)
+            for a in range(PASSES):
+                nc.vector.quantize_mx(
+                    out=codes[:, a, :].bitcast(FP8X4),
+                    scales=scales[:, a, :],
+                    in_=grouped[:, a, :, :].rearrange("p c j -> p (c j)"),
+                )
+            return codes, scales
+
+        def product(codes, scales, half, m, g):
+            bank = psum.tile([P, 2, HALF], F32, name="mm", tag="mm", bufs=4)
+            for s in range(2):
+                tok = slice(g * PAIR + s * TOK, g * PAIR + (s + 1) * TOK)
+                for a in range(PASSES):
+                    nc.tensor.matmul_mx(
+                        out=bank[:, s, :],
+                        lhsT=g_words[a][:, tok].bitcast(FP8X4),
+                        lhsT_scale=g_scales[SCALE_ROW[a] :, tok],
+                        rhs=codes[:, a, :].bitcast(FP8X4),
+                        rhs_scale=scales[:, a, :],
+                        start=(a == 0),
+                        stop=(a == PASSES - 1),
+                    )
+            prod = sbuf(f"prod{half}{m}{g}", [P, 2, HALF], F32)
+            nc.vector.tensor_tensor(
+                prod[:], bank[:], b_vals[m][:, 2 * g : 2 * g + 2, half * HALF : (half + 1) * HALF], MULT
+            )
+            return prod
+
+        h_tok = [sbuf(f"h_tok{g}", [P, 2, H], BF16) for g in range(PAIRS)]
+
+        def add_parts(real, imag, half, g):
+            nc.vector.tensor_tensor(h_tok[g][:, :, half * HALF : (half + 1) * HALF], real[:], imag[:], ADD)
+
+        def turn(g):
+            xt = psum.tile([P, 2, 2, TOK], F32, name="xt", tag="xt", bufs=2)
+            for s in range(2):
+                words = h_tok[g][:, s, :].bitcast(F32)
+                for u in range(2):
+                    nc.tensor.transpose(xt[:, s, u, :], words[:, u : H // 2 : 2], ident[:])
+            grouped = sbuf(f"h_bf{g}", [P, PAIR * PACK], BF16)
+            nc.scalar.copy(
+                out=grouped[:].bitcast(F32).rearrange("p (s r u) -> p s r u", s=2, u=2),
+                in_=xt[:].rearrange("p s u r -> p s r u"),
+            )
+            return grouped
+
+        def beams(grouped, g):
+            codes = sbuf(f"h_codes{g}", [P, PAIR], U32)
+            scales = sbuf(f"h_scales{g}", [P, PAIR], U8)
+            nc.vector.quantize_mx(out=codes[:].bitcast(FP8X4), scales=scales[:], in_=grouped[:])
+            result = sbuf(f"result{g}", [P, BEAM_TILES, PAIR], F32)
+            banks = [psum.tile([P, 2, PAIR], F32, name="y", tag="y", bufs=2) for b in range(2)]
+            for c in range(BEAM_TILES):
+                cols = slice(c * P, (c + 1) * P)
+                y = banks[c // 2][:, c % 2, :]
+                nc.tensor.matmul_mx(
+                    out=y,
+                    lhsT=bm_words[:, cols].bitcast(FP8X4),
+                    lhsT_scale=bm_scales[:].bitcast(U8)[:, cols],
+                    rhs=codes[:].bitcast(FP8X4),
+                    rhs_scale=scales[:],
+                    start=True,
+                    stop=True,
+                )
+            for c in range(BEAM_TILES):
+                nc.scalar.activation(
+                    out=result[:, c, :], in_=banks[c // 2][:, c % 2, :], func=IDENTITY,
+                    bias=base_cols[:, c : c + 1], scale=gain_cols[:, c : c + 1],
+                )
+            nc.sync.dma_start(
+                out=out[:, g * PAIR : (g + 1) * PAIR].rearrange("(c p) j -> p c j", p=P), in_=result[:]
+            )
+
+        rounded = {(0, 0): round_weights(nc.vector.tensor_copy, 0, 0)}
+        for half, m in ((0, 1), (1, 0), (1, 1)):
+            rounded[half, m] = round_weights(nc.scalar.copy, half, m)
+
+        real = {}
+        for half in range(2):
+            codes, scales = quantize_weights(rounded[half, 0], half, 0)
+            for g in range(PAIRS):
+                real[g] = product(codes, scales, half, 0, g)
+            codes, scales = quantize_weights(rounded[half, 1], half, 1)
+            imag = {}
+            turned = {}
+            for step in range(PAIRS + 2):
+                if step < PAIRS:
+                    imag[step] = product(codes, scales, half, 1, step)
+                if 1 <= step <= PAIRS:
+                    add_parts(real[step - 1], imag[step - 1], half, step - 1)
+                    if half == 1:
+                        turned[step - 1] = turn(step - 1)
+                if half == 1 and step >= 2:
+                    beams(turned[step - 2], step - 2)

@@ -59,15 +59,21 @@ def tile_list_reference_matched_beams_kernel(
         base_cols = sbuf("base_cols", [P, BEAM_TILES], F32)
         ident = sbuf("ident", [P, P], F32)
 
-        nc.vector.memset(v2_scales[:], 0)
-        nc.vector.memset(wb_scales[0][:], 0)
+        nc.gpsimd.memset(v2_scales[:], 0)
         nc.vector.memset(v_scales[:], 0)
+        nc.vector.memset(wb_scales[0][:], 0)
         nc.vector.memset(wb_scales[1][:], 0)
         nc.vector.memset(bm_scales[:], 0)
 
-        def load_scale_rows(queue, plane, rows):
-            for q in range(4):
-                queue.dma_start(out=plane[32 * q : 32 * q + 4, :], in_=rows[0, 4 * q : 4 * q + 4, :].bitcast(I32))
+        def load_scale_rows(plane, rows):
+            for r in range(4):
+                nc.sync.dma_start(out=plane[r:P:32, :], in_=rows[0, r:16:4, :].bitcast(I32))
+
+        def load_table_scales(queue, q):
+            queue.dma_start(
+                out=v_scales[32 * q + 4 : 32 * q + 12, :],
+                in_=tab_scales[:, 4 * q : 4 * q + 4, :].bitcast(I32),
+            )
 
         def words_of(dram, a):
             return dram[a].rearrange("p t i -> p (t i)").bitcast(I32)
@@ -77,21 +83,19 @@ def tile_list_reference_matched_beams_kernel(
             nc.sync.dma_start(out=v_words[a][:, cols], in_=words_of(tab_words, a)[:, cols])
 
         nc.sync.dma_start(idx2[:], offs2)
-        nc.sync.dma_start(out=v2_words[:], in_=words_of(tab2_words, 0))
-        load_scale_rows(nc.scalar, v2_scales, tab2_scales)
-        load_scale_rows(nc.scalar, wb_scales[0], wbr_scales)
-        for q in range(4):
-            nc.gpsimd.dma_start(
-                out=v_scales[32 * q + 4 : 32 * q + 12, :],
-                in_=tab_scales[:, 4 * q : 4 * q + 4, :].bitcast(I32),
-            )
         nc.sync.dma_start(out=wb_words[0][:], in_=wbr_words[0].bitcast(I32))
+        nc.sync.dma_start(out=v2_words[:], in_=words_of(tab2_words, 0))
+        load_scale_rows(v2_scales, tab2_scales)
+        for q in range(3):
+            load_table_scales(nc.gpsimd, q)
         load_table_half(0, 0)
+        load_scale_rows(wb_scales[0], wbr_scales)
         nc.sync.dma_start(idx[:], offs)
         load_table_half(0, 1)
         nc.sync.dma_start(out=wb_words[1][:], in_=wbi_words[0].bitcast(I32))
+        load_scale_rows(wb_scales[1], wbi_scales)
+        load_table_scales(nc.sync, 3)
         load_table_half(1, 0)
-        load_scale_rows(nc.sync, wb_scales[1], wbi_scales)
         load_table_half(1, 1)
 
         wa_raw = {}
@@ -103,7 +107,7 @@ def tile_list_reference_matched_beams_kernel(
                     nc.sync.dma_start(out=raw[:], in_=rows.rearrange("(p j) c -> p j c", j=PACK))
                     wa_raw[half, m, a] = raw
         nc.sync.dma_start(out=bm_words[:], in_=words_of(beam_words, 0))
-        load_scale_rows(nc.sync, bm_scales, beam_scales)
+        load_scale_rows(bm_scales, beam_scales)
         with nc.allow_non_contiguous_dma(reason="one gain and one baseline for each partition"):
             nc.sync.dma_start(out=gain_cols[:], in_=gain.rearrange("(c p) -> p c", p=P))
             nc.sync.dma_start(out=base_cols[:], in_=base.rearrange("(c p) -> p c", p=P))
@@ -117,19 +121,20 @@ def tile_list_reference_matched_beams_kernel(
         g2_words = sbuf("g2_words", [P, S], U32)
         g2_scales = sbuf("g2_scales", [P, S], U8)
 
-        for first in (0, S // 2):
-            gather(g2_words, v2_words[:].bitcast(U32), idx2, first, first + S // 2)
-            gather(g2_scales, v2_scales[:].bitcast(U8), idx2, first, first + S // 2)
+        for first, last in ((0, 256), (256, 512), (512, S)):
+            gather(g2_words, v2_words[:].bitcast(U32), idx2, first, last)
+            gather(g2_scales, v2_scales[:].bitcast(U8), idx2, first, last)
         gather(g_words[0], v_words[0][:].bitcast(U32), idx, 0, S)
         gather(g_scales, v_scales[:].bitcast(U8), idx, 0, S)
         for first in (0, S // 2):
             gather(g_words[1], v_words[1][:].bitcast(U32), idx, first, first + S // 2)
 
         b_vals = [sbuf(f"b_vals{m}", [P, TILES, H], F32) for m in range(2)]
-        for m in range(2):
+
+        def reference_channels(m):
             for j in range(TILES):
                 tok = slice(j * TOK, (j + 1) * TOK)
-                bank = psum.tile([P, H], F32, name="mm", tag="mm", bufs=4)
+                bank = psum.tile([P, H], F32, name="y", tag="y", bufs=3)
                 nc.tensor.matmul_mx(
                     out=bank[:],
                     lhsT=g2_words[:, tok].bitcast(FP8X4),
@@ -139,30 +144,34 @@ def tile_list_reference_matched_beams_kernel(
                     start=True,
                     stop=True,
                 )
-                nc.scalar.copy(out=b_vals[m][:, j, :], in_=bank[:])
-
-        def round_weights(copy, half, m):
-            grouped = sbuf(f"wa_bf{half}{m}", [P, PASSES, HALF, PACK], BF16)
-            for a in range(PASSES):
-                copy(
-                    out=grouped[:, a, :, :].rearrange("p (c i) j -> p c j i", i=4),
-                    in_=wa_raw[half, m, a][:].rearrange("p j (c i) -> p c j i", i=4),
+                nc.scalar.copy(
+                    out=b_vals[m][:, j, :].rearrange("p (h u q e) -> p h u q e", h=2, u=2, e=2),
+                    in_=bank[:].rearrange("p (h q u e) -> p h u q e", h=2, u=2, e=2),
                 )
-            return grouped
 
-        def quantize_weights(grouped, half, m):
+        wa_bf = {
+            (half, m): sbuf(f"wa_bf{half}{m}", [P, PASSES, HALF, PACK], BF16) for half in range(2) for m in range(2)
+        }
+
+        def round_weights(copy, half, m, a):
+            copy(
+                out=wa_bf[half, m][:, a, :, :].rearrange("p (u q e) j -> p q j u e", u=2, e=2),
+                in_=wa_raw[half, m, a][:].rearrange("p j (q u e) -> p q j u e", u=2, e=2),
+            )
+
+        def quantize_weights(half, m, calls):
             codes = sbuf(f"wa_codes{half}{m}", [P, PASSES, HALF], U32)
             scales = sbuf(f"wa_scales{half}{m}", [P, PASSES, HALF], U8)
-            for a in range(PASSES):
+            for passes in calls:
                 nc.vector.quantize_mx(
-                    out=codes[:, a, :].bitcast(FP8X4),
-                    scales=scales[:, a, :],
-                    in_=grouped[:, a, :, :].rearrange("p c j -> p (c j)"),
+                    out=codes[:, passes, :].rearrange("p a c -> p (a c)").bitcast(FP8X4),
+                    scales=scales[:, passes, :].rearrange("p a c -> p (a c)"),
+                    in_=wa_bf[half, m][:, passes, :, :].rearrange("p a c j -> p (a c j)"),
                 )
             return codes, scales
 
         def product(codes, scales, half, m, g):
-            bank = psum.tile([P, 2, HALF], F32, name="mm", tag="mm", bufs=4)
+            bank = psum.tile([P, 2, HALF], F32, name="mm", tag="mm", bufs=3)
             for s in range(2):
                 tok = slice(g * PAIR + s * TOK, g * PAIR + (s + 1) * TOK)
                 for a in range(PASSES):
@@ -183,33 +192,41 @@ def tile_list_reference_matched_beams_kernel(
 
         h_tok = [sbuf(f"h_tok{g}", [P, 2, H], BF16) for g in range(PAIRS)]
 
-        def add_parts(real, imag, half, g):
-            nc.vector.tensor_tensor(h_tok[g][:, :, half * HALF : (half + 1) * HALF], real[:], imag[:], ADD)
+        def add_parts(engine, real, imag, half, g, tiles):
+            engine.tensor_tensor(
+                h_tok[g][:, tiles, :].rearrange("p s (u h x) -> p s u h x", u=2, h=2)[:, :, :, half, :],
+                real[:, tiles, :].rearrange("p s (u x) -> p s u x", u=2),
+                imag[:, tiles, :].rearrange("p s (u x) -> p s u x", u=2),
+                ADD,
+            )
 
-        def turn(g):
-            xt = psum.tile([P, 2, 2, TOK], F32, name="xt", tag="xt", bufs=2)
-            for s in range(2):
-                words = h_tok[g][:, s, :].bitcast(F32)
+        def turn(g, tiles):
+            count = tiles.stop - tiles.start
+            xt = psum.tile([P, count, 2, TOK], F32, name="xt", tag="xt", bufs=2)
+            for s in range(count):
+                words = h_tok[g][:, tiles.start + s, :].bitcast(F32)
                 for u in range(2):
-                    nc.tensor.transpose(xt[:, s, u, :], words[:, u : H // 2 : 2], ident[:])
-            grouped = sbuf(f"h_bf{g}", [P, PAIR * PACK], BF16)
+                    nc.tensor.transpose(xt[:, s, u, :], words[:, u * P : (u + 1) * P], ident[:])
+            grouped = sbuf(f"h_bf{g}{tiles.start}", [P, count * TOK * PACK], BF16)
             nc.scalar.copy(
-                out=grouped[:].bitcast(F32).rearrange("p (s r u) -> p s r u", s=2, u=2),
+                out=grouped[:].bitcast(F32).rearrange("p (s r u) -> p s r u", s=count, u=2),
                 in_=xt[:].rearrange("p s u r -> p s r u"),
             )
             return grouped
 
-        def beams(grouped, g):
-            codes = sbuf(f"h_codes{g}", [P, PAIR], U32)
-            scales = sbuf(f"h_scales{g}", [P, PAIR], U8)
+        def beams(grouped, g, tiles, last):
+            width = (tiles.stop - tiles.start) * TOK
+            first = g * PAIR + tiles.start * TOK
+            codes = sbuf(f"h_codes{first}", [P, width], U32)
+            scales = sbuf(f"h_scales{first}", [P, width], U8)
             nc.vector.quantize_mx(out=codes[:].bitcast(FP8X4), scales=scales[:], in_=grouped[:])
-            result = sbuf(f"result{g}", [P, BEAM_TILES, PAIR], F32)
-            banks = [psum.tile([P, 2, PAIR], F32, name="y", tag="y", bufs=2) for b in range(2)]
+            result = sbuf(f"result{first}", [P, BEAM_TILES, width], F32)
+            rows = out[:, first : first + width].rearrange("(c p) j -> p c j", p=P)
             for c in range(BEAM_TILES):
                 cols = slice(c * P, (c + 1) * P)
-                y = banks[c // 2][:, c % 2, :]
+                y = psum.tile([P, width], F32, name="y", tag="y", bufs=3)
                 nc.tensor.matmul_mx(
-                    out=y,
+                    out=y[:],
                     lhsT=bm_words[:, cols].bitcast(FP8X4),
                     lhsT_scale=bm_scales[:].bitcast(U8)[:, cols],
                     rhs=codes[:].bitcast(FP8X4),
@@ -217,33 +234,59 @@ def tile_list_reference_matched_beams_kernel(
                     start=True,
                     stop=True,
                 )
-            for c in range(BEAM_TILES):
-                nc.scalar.activation(
-                    out=result[:, c, :], in_=banks[c // 2][:, c % 2, :], func=IDENTITY,
-                    bias=base_cols[:, c : c + 1], scale=gain_cols[:, c : c + 1],
-                )
-            nc.sync.dma_start(
-                out=out[:, g * PAIR : (g + 1) * PAIR].rearrange("(c p) j -> p c j", p=P), in_=result[:]
-            )
+                if last and c == 1:
+                    nc.vector.tensor_scalar(
+                        out=result[:, c, :], in0=y[:], scalar1=gain_cols[:, c : c + 1],
+                        scalar2=base_cols[:, c : c + 1], op0=MULT, op1=ADD,
+                    )
+                else:
+                    nc.scalar.activation(
+                        out=result[:, c, :], in_=y[:], func=IDENTITY,
+                        bias=base_cols[:, c : c + 1], scale=gain_cols[:, c : c + 1],
+                    )
+            nc.sync.dma_start(out=rows, in_=result[:])
 
-        rounded = {(0, 0): round_weights(nc.vector.tensor_copy, 0, 0)}
+        reference_channels(0)
+        reference_channels(1)
+        for a in range(PASSES):
+            round_weights(nc.vector.tensor_copy, 0, 0, a)
         for half, m in ((0, 1), (1, 0), (1, 1)):
-            rounded[half, m] = round_weights(nc.scalar.copy, half, m)
+            for a in range(PASSES):
+                round_weights(nc.scalar.copy, half, m, a)
 
-        real = {}
-        for half in range(2):
-            codes, scales = quantize_weights(rounded[half, 0], half, 0)
-            for g in range(PAIRS):
-                real[g] = product(codes, scales, half, 0, g)
-            codes, scales = quantize_weights(rounded[half, 1], half, 1)
-            imag = {}
-            turned = {}
-            for step in range(PAIRS + 2):
-                if step < PAIRS:
-                    imag[step] = product(codes, scales, half, 1, step)
-                if 1 <= step <= PAIRS:
-                    add_parts(real[step - 1], imag[step - 1], half, step - 1)
-                    if half == 1:
-                        turned[step - 1] = turn(step - 1)
-                if half == 1 and step >= 2:
-                    beams(turned[step - 2], step - 2)
+        by_pass = [slice(a, a + 1) for a in range(PASSES)]
+        whole = [slice(0, PASSES)]
+        both = slice(0, 2)
+        single = [slice(0, 1), slice(1, 2)]
+
+        weights = {(0, 0): quantize_weights(0, 0, by_pass)}
+
+        def products(half, m, following):
+            parts = [product(*weights[half, m], half, m, g) for g in range(PAIRS - 1)]
+            weights[following] = quantize_weights(*following, whole)
+            return parts + [product(*weights[half, m], half, m, PAIRS - 1)]
+
+        real = products(0, 0, (0, 1))
+        imag = products(0, 1, (1, 0))
+        for g in range(PAIRS):
+            for tiles in single:
+                add_parts(nc.gpsimd, real[g], imag[g], 0, g, tiles)
+
+        real = product(*weights[1, 0], 1, 0, 0)
+        weights[1, 1] = quantize_weights(1, 1, whole)
+        imag = product(*weights[1, 1], 1, 1, 0)
+        turned = {}
+        for g in range(PAIRS - 1):
+            following = product(*weights[1, 0], 1, 0, g + 1)
+            add_parts(nc.vector, real, imag, 1, g, both)
+            turned[g] = turn(g, both)
+            real, imag = following, product(*weights[1, 1], 1, 1, g + 1)
+            if g >= 1:
+                beams(turned[g - 1], g - 1, both, False)
+        ends = []
+        for tiles in single:
+            add_parts(nc.vector, real, imag, 1, PAIRS - 1, tiles)
+            ends.append(turn(PAIRS - 1, tiles))
+        beams(turned[PAIRS - 2], PAIRS - 2, both, True)
+        for tiles, grouped in zip(single, ends):
+            beams(grouped, PAIRS - 1, tiles, True)

@@ -84,13 +84,14 @@ def tile_list_reference_matched_beams_kernel(
 
         nc.sync.dma_start(idx2[:], offs2)
         nc.sync.dma_start(out=wb_words[0][:], in_=wbr_words[0].bitcast(I32))
-        nc.sync.dma_start(out=v2_words[:], in_=words_of(tab2_words, 0))
+        nc.sync.dma_start(out=v2_words[:, : T2 // 2], in_=words_of(tab2_words, 0)[:, : T2 // 2])
         load_scale_rows(v2_scales, tab2_scales)
+        nc.sync.dma_start(out=v2_words[:, T2 // 2 :], in_=words_of(tab2_words, 0)[:, T2 // 2 :])
+        load_scale_rows(wb_scales[0], wbr_scales)
         for q in range(3):
             load_table_scales(nc.gpsimd, q)
-        load_table_half(0, 0)
-        load_scale_rows(wb_scales[0], wbr_scales)
         nc.sync.dma_start(idx[:], offs)
+        load_table_half(0, 0)
         load_table_half(0, 1)
         nc.sync.dma_start(out=wb_words[1][:], in_=wbi_words[0].bitcast(I32))
         load_scale_rows(wb_scales[1], wbi_scales)
@@ -99,13 +100,13 @@ def tile_list_reference_matched_beams_kernel(
         load_table_half(1, 1)
 
         wa_raw = {}
-        for half in range(2):
-            for m, w in enumerate((war, wai)):
-                for a in range(PASSES):
-                    raw = sbuf(f"wa_raw{half}{m}{a}", [P, PACK, HALF], F32)
-                    rows = w[a * K_PASS : (a + 1) * K_PASS, half * HALF : (half + 1) * HALF]
-                    nc.sync.dma_start(out=raw[:], in_=rows.rearrange("(p j) c -> p j c", j=PACK))
-                    wa_raw[half, m, a] = raw
+        low = [(0, m, a) for m in range(2) for a in range(PASSES)]
+        high = [(1, m, a) for a in range(PASSES) for m in range(2)]
+        for half, m, a in low + high:
+            raw = sbuf(f"wa_raw{half}{m}{a}", [P, PACK, HALF], F32)
+            rows = (war, wai)[m][a * K_PASS : (a + 1) * K_PASS, half * HALF : (half + 1) * HALF]
+            nc.sync.dma_start(out=raw[:], in_=rows.rearrange("(p j) c -> p j c", j=PACK))
+            wa_raw[half, m, a] = raw
         nc.sync.dma_start(out=bm_words[:], in_=words_of(beam_words, 0))
         load_scale_rows(bm_scales, beam_scales)
         with nc.allow_non_contiguous_dma(reason="one gain and one baseline for each partition"):
@@ -121,15 +122,15 @@ def tile_list_reference_matched_beams_kernel(
         g2_words = sbuf("g2_words", [P, S], U32)
         g2_scales = sbuf("g2_scales", [P, S], U8)
 
+        gather(g2_scales, v2_scales[:].bitcast(U8), idx2, 0, S)
         for first, last in ((0, 256), (256, 512), (512, S)):
             gather(g2_words, v2_words[:].bitcast(U32), idx2, first, last)
-            gather(g2_scales, v2_scales[:].bitcast(U8), idx2, first, last)
         gather(g_words[0], v_words[0][:].bitcast(U32), idx, 0, S)
         gather(g_scales, v_scales[:].bitcast(U8), idx, 0, S)
         for first in (0, S // 2):
             gather(g_words[1], v_words[1][:].bitcast(U32), idx, first, first + S // 2)
 
-        b_vals = [sbuf(f"b_vals{m}", [P, TILES, H], F32) for m in range(2)]
+        b_vals = sbuf("b_vals", [P, 2, TILES, H], F32)
 
         def reference_channels(m):
             for j in range(TILES):
@@ -145,13 +146,14 @@ def tile_list_reference_matched_beams_kernel(
                     stop=True,
                 )
                 nc.scalar.copy(
-                    out=b_vals[m][:, j, :].rearrange("p (h u q e) -> p h u q e", h=2, u=2, e=2),
+                    out=b_vals[:, m, j, :].rearrange("p (h u q e) -> p h u q e", h=2, u=2, e=2),
                     in_=bank[:].rearrange("p (h q u e) -> p h u q e", h=2, u=2, e=2),
                 )
 
-        wa_bf = {
-            (half, m): sbuf(f"wa_bf{half}{m}", [P, PASSES, HALF, PACK], BF16) for half in range(2) for m in range(2)
-        }
+        wa_bf = {(0, m): sbuf(f"wa_bf0{m}", [P, PASSES, HALF, PACK], BF16) for m in range(2)}
+        high_bf = sbuf("high_bf", [P, PASSES, 2, HALF, PACK], BF16)
+        for m in range(2):
+            wa_bf[1, m] = high_bf[:, :, m]
 
         def round_weights(copy, half, m, a):
             copy(
@@ -186,9 +188,41 @@ def tile_list_reference_matched_beams_kernel(
                     )
             prod = sbuf(f"prod{half}{m}{g}", [P, 2, HALF], F32)
             nc.vector.tensor_tensor(
-                prod[:], bank[:], b_vals[m][:, 2 * g : 2 * g + 2, half * HALF : (half + 1) * HALF], MULT
+                prod[:], bank[:], b_vals[:, m, 2 * g : 2 * g + 2, :HALF], MULT
             )
             return prod
+
+        high_codes = sbuf("high_codes", [P, PASSES, H], U32)
+        high_scales = sbuf("high_scales", [P, PASSES, H], U8)
+
+        def quantize_high(a):
+            nc.vector.quantize_mx(
+                out=high_codes[:, a, :].bitcast(FP8X4),
+                scales=high_scales[:, a, :],
+                in_=high_bf[:, a].rearrange("p m c j -> p (m c j)"),
+            )
+
+        high_parts = [sbuf(f"high_parts{g}", [P, 2, 2, HALF], F32) for g in range(PAIRS)]
+
+        def product_high(j):
+            tok = slice(j * TOK, (j + 1) * TOK)
+            bank = psum.tile([P, H], F32, name="mm", tag="mm", bufs=3)
+            for a in range(PASSES):
+                nc.tensor.matmul_mx(
+                    out=bank[:],
+                    lhsT=g_words[a][:, tok].bitcast(FP8X4),
+                    lhsT_scale=g_scales[SCALE_ROW[a] :, tok],
+                    rhs=high_codes[:, a, :].bitcast(FP8X4),
+                    rhs_scale=high_scales[:, a, :],
+                    start=(a == 0),
+                    stop=(a == PASSES - 1),
+                )
+            nc.vector.tensor_tensor(
+                high_parts[j // 2][:, :, j % 2, :],
+                bank[:].rearrange("p (m c) -> p m c", m=2),
+                b_vals[:, :, j, HALF:],
+                MULT,
+            )
 
         h_tok = [sbuf(f"h_tok{g}", [P, 2, H], BF16) for g in range(PAIRS)]
 
@@ -248,11 +282,23 @@ def tile_list_reference_matched_beams_kernel(
 
         reference_channels(0)
         reference_channels(1)
-        for a in range(PASSES):
-            round_weights(nc.vector.tensor_copy, 0, 0, a)
-        for half, m in ((0, 1), (1, 0), (1, 1)):
-            for a in range(PASSES):
-                round_weights(nc.scalar.copy, half, m, a)
+        unread = psum.tile([P, H], F32, name="xt", tag="xt", bufs=2)
+        for first, count in ((0, 2), (S // 2, 3)):
+            for repeat in range(count):
+                tok = slice(first + repeat * TOK, first + (repeat + 1) * TOK)
+                nc.tensor.matmul_mx(
+                    out=unread[:],
+                    lhsT=g_words[1][:, tok].bitcast(FP8X4),
+                    lhsT_scale=g_scales[SCALE_ROW[1] :, tok],
+                    rhs=g2_words[:, :H].bitcast(FP8X4),
+                    rhs_scale=g2_scales[:, :H],
+                    start=True,
+                    stop=True,
+                )
+        round_weights(nc.scalar.copy, 0, 0, 0)
+        round_weights(nc.vector.tensor_copy, 0, 0, 1)
+        for half, m, a in low[2:] + high:
+            round_weights(nc.scalar.copy, half, m, a)
 
         by_pass = [slice(a, a + 1) for a in range(PASSES)]
         whole = [slice(0, PASSES)]
@@ -261,31 +307,31 @@ def tile_list_reference_matched_beams_kernel(
 
         weights = {(0, 0): quantize_weights(0, 0, by_pass)}
 
-        def products(half, m, following):
-            parts = [product(*weights[half, m], half, m, g) for g in range(PAIRS - 1)]
-            weights[following] = quantize_weights(*following, whole)
-            return parts + [product(*weights[half, m], half, m, PAIRS - 1)]
-
-        real = products(0, 0, (0, 1))
-        imag = products(0, 1, (1, 0))
+        real = [product(*weights[0, 0], 0, 0, g) for g in range(PAIRS - 1)]
+        weights[0, 1] = quantize_weights(0, 1, whole)
+        real.append(product(*weights[0, 0], 0, 0, PAIRS - 1))
+        imag = [product(*weights[0, 1], 0, 1, g) for g in range(2)]
+        quantize_high(0)
+        imag.append(product(*weights[0, 1], 0, 1, 2))
+        quantize_high(1)
+        imag.append(product(*weights[0, 1], 0, 1, 3))
         for g in range(PAIRS):
             for tiles in single:
                 add_parts(nc.gpsimd, real[g], imag[g], 0, g, tiles)
 
-        real = product(*weights[1, 0], 1, 0, 0)
-        weights[1, 1] = quantize_weights(1, 1, whole)
-        imag = product(*weights[1, 1], 1, 1, 0)
+        product_high(0)
+        product_high(1)
         turned = {}
         for g in range(PAIRS - 1):
-            following = product(*weights[1, 0], 1, 0, g + 1)
-            add_parts(nc.vector, real, imag, 1, g, both)
+            product_high(2 * g + 2)
+            add_parts(nc.vector, high_parts[g][:, 0], high_parts[g][:, 1], 1, g, both)
             turned[g] = turn(g, both)
-            real, imag = following, product(*weights[1, 1], 1, 1, g + 1)
+            product_high(2 * g + 3)
             if g >= 1:
                 beams(turned[g - 1], g - 1, both, False)
         ends = []
         for tiles in single:
-            add_parts(nc.vector, real, imag, 1, PAIRS - 1, tiles)
+            add_parts(nc.vector, high_parts[PAIRS - 1][:, 0], high_parts[PAIRS - 1][:, 1], 1, PAIRS - 1, tiles)
             ends.append(turn(PAIRS - 1, tiles))
         beams(turned[PAIRS - 2], PAIRS - 2, both, True)
         for tiles, grouped in zip(single, ends):

@@ -78,8 +78,8 @@ def tile_list_reference_matched_beams_kernel(
         def words_of(dram, a):
             return dram[a].rearrange("p t i -> p (t i)").bitcast(I32)
 
-        def load_table_half(a, u):
-            cols = slice(u * T // 2, (u + 1) * T // 2)
+        def load_table(a, first, last):
+            cols = slice(first, last)
             nc.sync.dma_start(out=v_words[a][:, cols], in_=words_of(tab_words, a)[:, cols])
 
         nc.sync.dma_start(idx2[:], offs2)
@@ -87,22 +87,23 @@ def tile_list_reference_matched_beams_kernel(
         nc.sync.dma_start(out=v2_words[:, : T2 // 2], in_=words_of(tab2_words, 0)[:, : T2 // 2])
         load_scale_rows(v2_scales, tab2_scales)
         nc.sync.dma_start(out=v2_words[:, T2 // 2 :], in_=words_of(tab2_words, 0)[:, T2 // 2 :])
+        load_table(0, 0, T // 4)
         load_scale_rows(wb_scales[0], wbr_scales)
         for q in range(3):
             load_table_scales(nc.gpsimd, q)
         nc.sync.dma_start(idx[:], offs)
-        load_table_half(0, 0)
-        load_table_half(0, 1)
+        load_table(0, T // 4, T)
         nc.sync.dma_start(out=wb_words[1][:], in_=wbi_words[0].bitcast(I32))
         load_scale_rows(wb_scales[1], wbi_scales)
         load_table_scales(nc.sync, 3)
-        load_table_half(1, 0)
-        load_table_half(1, 1)
 
         wa_raw = {}
         low = [(0, m, a) for m in range(2) for a in range(PASSES)]
         high = [(1, m, a) for a in range(PASSES) for m in range(2)]
         for half, m, a in low + high:
+            if (half, m, a) == (0, 1, 0):
+                load_table(1, 0, T // 2)
+                load_table(1, T // 2, T)
             raw = sbuf(f"wa_raw{half}{m}{a}", [P, PACK, HALF], F32)
             rows = (war, wai)[m][a * K_PASS : (a + 1) * K_PASS, half * HALF : (half + 1) * HALF]
             nc.sync.dma_start(out=raw[:], in_=rows.rearrange("(p j) c -> p j c", j=PACK))
@@ -127,8 +128,6 @@ def tile_list_reference_matched_beams_kernel(
             gather(g2_words, v2_words[:].bitcast(U32), idx2, first, last)
         gather(g_words[0], v_words[0][:].bitcast(U32), idx, 0, S)
         gather(g_scales, v_scales[:].bitcast(U8), idx, 0, S)
-        for first in (0, S // 2):
-            gather(g_words[1], v_words[1][:].bitcast(U32), idx, first, first + S // 2)
 
         b_vals = sbuf("b_vals", [P, 2, TILES, H], F32)
 
@@ -174,17 +173,17 @@ def tile_list_reference_matched_beams_kernel(
 
         def product(codes, scales, half, m, g):
             bank = psum.tile([P, 2, HALF], F32, name="mm", tag="mm", bufs=3)
-            for s in range(2):
-                tok = slice(g * PAIR + s * TOK, g * PAIR + (s + 1) * TOK)
-                for a in range(PASSES):
+            for a in range(PASSES):
+                for s in range(2):
+                    tok = slice(g * PAIR + s * TOK, g * PAIR + (s + 1) * TOK)
                     nc.tensor.matmul_mx(
                         out=bank[:, s, :],
                         lhsT=g_words[a][:, tok].bitcast(FP8X4),
                         lhsT_scale=g_scales[SCALE_ROW[a] :, tok],
                         rhs=codes[:, a, :].bitcast(FP8X4),
                         rhs_scale=scales[:, a, :],
-                        start=(a == 0),
-                        stop=(a == PASSES - 1),
+                        start=(a == 0 and s == 0),
+                        stop=(a == PASSES - 1 and s == 1),
                     )
             prod = sbuf(f"prod{half}{m}{g}", [P, 2, HALF], F32)
             nc.vector.tensor_tensor(
@@ -282,30 +281,18 @@ def tile_list_reference_matched_beams_kernel(
 
         reference_channels(0)
         reference_channels(1)
-        unread = psum.tile([P, H], F32, name="xt", tag="xt", bufs=2)
-        for first, count in ((0, 2), (S // 2, 3)):
-            for repeat in range(count):
-                tok = slice(first + repeat * TOK, first + (repeat + 1) * TOK)
-                nc.tensor.matmul_mx(
-                    out=unread[:],
-                    lhsT=g_words[1][:, tok].bitcast(FP8X4),
-                    lhsT_scale=g_scales[SCALE_ROW[1] :, tok],
-                    rhs=g2_words[:, :H].bitcast(FP8X4),
-                    rhs_scale=g2_scales[:, :H],
-                    start=True,
-                    stop=True,
-                )
-        round_weights(nc.scalar.copy, 0, 0, 0)
-        round_weights(nc.vector.tensor_copy, 0, 0, 1)
+        for a in range(PASSES):
+            round_weights(nc.vector.tensor_copy, 0, 0, a)
         for half, m, a in low[2:] + high:
             round_weights(nc.scalar.copy, half, m, a)
 
-        by_pass = [slice(a, a + 1) for a in range(PASSES)]
         whole = [slice(0, PASSES)]
         both = slice(0, 2)
         single = [slice(0, 1), slice(1, 2)]
 
-        weights = {(0, 0): quantize_weights(0, 0, by_pass)}
+        weights = {(0, 0): quantize_weights(0, 0, whole)}
+        for first in (0, S // 2):
+            gather(g_words[1], v_words[1][:].bitcast(U32), idx, first, first + S // 2)
 
         real = [product(*weights[0, 0], 0, 0, g) for g in range(PAIRS - 1)]
         weights[0, 1] = quantize_weights(0, 1, whole)

@@ -89,13 +89,12 @@ def tile_list_reference_matched_beams_kernel(
         nc.sync.dma_start(out=v2_words[:, T2 // 2 :], in_=words_of(tab2_words, 0)[:, T2 // 2 :])
         load_table(0, 0, T // 4)
         load_scale_rows(wb_scales[0], wbr_scales)
-        for q in range(3):
+        for q in range(4):
             load_table_scales(nc.gpsimd, q)
         nc.sync.dma_start(idx[:], offs)
         load_table(0, T // 4, T)
         nc.sync.dma_start(out=wb_words[1][:], in_=wbi_words[0].bitcast(I32))
         load_scale_rows(wb_scales[1], wbi_scales)
-        load_table_scales(nc.sync, 3)
 
         wa_raw = {}
         low = [(0, m, a) for m in range(2) for a in range(PASSES)]
@@ -277,7 +276,11 @@ def tile_list_reference_matched_beams_kernel(
                         out=result[:, c, :], in_=y[:], func=IDENTITY,
                         bias=base_cols[:, c : c + 1], scale=gain_cols[:, c : c + 1],
                     )
-            nc.sync.dma_start(out=rows, in_=result[:])
+            if first + width == S:
+                nc.sync.dma_start(out=rows[:, :2, :], in_=result[:, :2, :])
+                nc.scalar.dma_start(out=rows[:, 2, :], in_=result[:, 2, :])
+            else:
+                nc.sync.dma_start(out=rows, in_=result[:])
 
         reference_channels(0)
         reference_channels(1)

@@ -29,6 +29,7 @@ PAIRS = S // PAIR
 HALF = H // 2
 BEAM_TILES = N // P
 SCALE_ROW = (4, 8)
+SUMMED_IN_PSUM = (0, 3)
 
 
 def tile_list_reference_matched_beams_kernel(
@@ -97,16 +98,16 @@ def tile_list_reference_matched_beams_kernel(
         load_scale_rows(wb_scales[1], wbi_scales)
 
         wa_raw = {}
-        low = [(0, m, a) for m in range(2) for a in range(PASSES)]
-        high = [(1, m, a) for a in range(PASSES) for m in range(2)]
-        for half, m, a in low + high:
-            if (half, m, a) == (0, 1, 0):
+        pieces = [(0, 0), (0, 1), (1, 0), (1, 1)]
+        for m, half in pieces:
+            if (m, half) == (0, 1):
                 load_table(1, 0, T // 2)
                 load_table(1, T // 2, T)
-            raw = sbuf(f"wa_raw{half}{m}{a}", [P, PACK, HALF], F32)
-            rows = (war, wai)[m][a * K_PASS : (a + 1) * K_PASS, half * HALF : (half + 1) * HALF]
-            nc.sync.dma_start(out=raw[:], in_=rows.rearrange("(p j) c -> p j c", j=PACK))
-            wa_raw[half, m, a] = raw
+            for a in range(PASSES):
+                raw = sbuf(f"wa_raw{m}{half}{a}", [P, PACK, HALF], F32)
+                rows = (war, wai)[m][a * K_PASS : (a + 1) * K_PASS, half * HALF : (half + 1) * HALF]
+                nc.sync.dma_start(out=raw[:], in_=rows.rearrange("(p j) c -> p j c", j=PACK))
+                wa_raw[m, half, a] = raw
         nc.sync.dma_start(out=bm_words[:], in_=words_of(beam_words, 0))
         load_scale_rows(bm_scales, beam_scales)
         with nc.allow_non_contiguous_dma(reason="one gain and one baseline for each partition"):
@@ -128,14 +129,17 @@ def tile_list_reference_matched_beams_kernel(
         gather(g_words[0], v_words[0][:].bitcast(U32), idx, 0, S)
         gather(g_scales, v_scales[:].bitcast(U8), idx, 0, S)
 
+        def bank(n, shape):
+            return psum.tile(shape, F32, name=f"bank{n}", tag=f"bank{n}", bufs=1)
+
         b_vals = sbuf("b_vals", [P, 2, TILES, H], F32)
 
         def reference_channels(m):
             for j in range(TILES):
                 tok = slice(j * TOK, (j + 1) * TOK)
-                bank = psum.tile([P, H], F32, name="y", tag="y", bufs=3)
+                acc = bank(5 + (m * TILES + j) % 3, [P, H])
                 nc.tensor.matmul_mx(
-                    out=bank[:],
+                    out=acc[:],
                     lhsT=g2_words[:, tok].bitcast(FP8X4),
                     lhsT_scale=g2_scales[:, tok],
                     rhs=wb_words[m][:].bitcast(U8).bitcast(FP4X4),
@@ -143,40 +147,51 @@ def tile_list_reference_matched_beams_kernel(
                     start=True,
                     stop=True,
                 )
-                nc.scalar.copy(
-                    out=b_vals[:, m, j, :].rearrange("p (h u q e) -> p h u q e", h=2, u=2, e=2),
-                    in_=bank[:].rearrange("p (h q u e) -> p h u q e", h=2, u=2, e=2),
-                )
+                if j // 2 in SUMMED_IN_PSUM:
+                    nc.scalar.copy(
+                        out=b_vals[:, m, j, :].rearrange("p (t q) -> p t q", t=PACK),
+                        in_=acc[:].rearrange("p (q t) -> p t q", t=PACK),
+                    )
+                else:
+                    nc.scalar.copy(out=b_vals[:, m, j, :], in_=acc[:])
 
-        wa_bf = {(0, m): sbuf(f"wa_bf0{m}", [P, PASSES, HALF, PACK], BF16) for m in range(2)}
-        high_bf = sbuf("high_bf", [P, PASSES, 2, HALF, PACK], BF16)
-        for m in range(2):
-            wa_bf[1, m] = high_bf[:, :, m]
+        wa_bf = {}
 
-        def round_weights(copy, half, m, a):
+        def stage(m, half, tag):
+            wa_bf[m, half] = keep.tile([P, PASSES, HALF, PACK], BF16, name=f"wa_bf{m}{half}", tag=tag, bufs=1, align_bytes=64)
+
+        def round_weights(copy, m, half, a):
             copy(
-                out=wa_bf[half, m][:, a, :, :].rearrange("p (u q e) j -> p q j u e", u=2, e=2),
-                in_=wa_raw[half, m, a][:].rearrange("p j (q u e) -> p q j u e", u=2, e=2),
+                out=wa_bf[m, half][:, a, :, :].rearrange("p (q t) j -> p q j t", t=PACK),
+                in_=wa_raw[m, half, a][:].rearrange("p j (q t) -> p q j t", t=PACK),
             )
 
-        def quantize_weights(half, m, calls):
-            codes = sbuf(f"wa_codes{half}{m}", [P, PASSES, HALF], U32)
-            scales = sbuf(f"wa_scales{half}{m}", [P, PASSES, HALF], U8)
-            for passes in calls:
-                nc.vector.quantize_mx(
-                    out=codes[:, passes, :].rearrange("p a c -> p (a c)").bitcast(FP8X4),
-                    scales=scales[:, passes, :].rearrange("p a c -> p (a c)"),
-                    in_=wa_bf[half, m][:, passes, :, :].rearrange("p a c j -> p (a c j)"),
-                )
-            return codes, scales
+        weights = {}
 
-        def product(codes, scales, half, m, g):
-            bank = psum.tile([P, 2, HALF], F32, name="mm", tag="mm", bufs=3)
-            for a in range(PASSES):
+        def quantize_weights(m, half):
+            codes = sbuf(f"wa_codes{m}{half}", [P, PASSES, HALF], U32)
+            scales = sbuf(f"wa_scales{m}{half}", [P, PASSES, HALF], U8)
+            nc.vector.quantize_mx(
+                out=codes[:].rearrange("p a c -> p (a c)").bitcast(FP8X4),
+                scales=scales[:].rearrange("p a c -> p (a c)"),
+                in_=wa_bf[m, half][:].rearrange("p a c j -> p (a c j)"),
+            )
+            weights[m, half] = codes, scales
+
+        parts = {(m, g): sbuf(f"parts{m}{g}", [P, 2, H], F32) for m in range(2) for g in range(PAIRS) if (m, g) != (0, 2)}
+
+        accs = {}
+
+        def accumulate(m, half, g, n, passes):
+            codes, scales = weights[m, half]
+            if 0 in passes:
+                accs[m, half, g] = bank(n, [P, 2, HALF])
+            acc = accs[m, half, g]
+            for a in passes:
                 for s in range(2):
                     tok = slice(g * PAIR + s * TOK, g * PAIR + (s + 1) * TOK)
                     nc.tensor.matmul_mx(
-                        out=bank[:, s, :],
+                        out=acc[:, s, :],
                         lhsT=g_words[a][:, tok].bitcast(FP8X4),
                         lhsT_scale=g_scales[SCALE_ROW[a] :, tok],
                         rhs=codes[:, a, :].bitcast(FP8X4),
@@ -184,81 +199,81 @@ def tile_list_reference_matched_beams_kernel(
                         start=(a == 0 and s == 0),
                         stop=(a == PASSES - 1 and s == 1),
                     )
-            prod = sbuf(f"prod{half}{m}{g}", [P, 2, HALF], F32)
-            nc.vector.tensor_tensor(
-                prod[:], bank[:], b_vals[:, m, 2 * g : 2 * g + 2, :HALF], MULT
-            )
-            return prod
 
-        high_codes = sbuf("high_codes", [P, PASSES, H], U32)
-        high_scales = sbuf("high_scales", [P, PASSES, H], U8)
-
-        def quantize_high(a):
-            nc.vector.quantize_mx(
-                out=high_codes[:, a, :].bitcast(FP8X4),
-                scales=high_scales[:, a, :],
-                in_=high_bf[:, a].rearrange("p m c j -> p (m c j)"),
-            )
-
-        high_parts = [sbuf(f"high_parts{g}", [P, 2, 2, HALF], F32) for g in range(PAIRS)]
-
-        def product_high(j):
-            tok = slice(j * TOK, (j + 1) * TOK)
-            bank = psum.tile([P, H], F32, name="mm", tag="mm", bufs=3)
-            for a in range(PASSES):
-                nc.tensor.matmul_mx(
-                    out=bank[:],
-                    lhsT=g_words[a][:, tok].bitcast(FP8X4),
-                    lhsT_scale=g_scales[SCALE_ROW[a] :, tok],
-                    rhs=high_codes[:, a, :].bitcast(FP8X4),
-                    rhs_scale=high_scales[:, a, :],
-                    start=(a == 0),
-                    stop=(a == PASSES - 1),
+        def product(m, half, g, n):
+            accumulate(m, half, g, n, [1] if (m, half, g) in accs else [0, 1])
+            acc = accs[m, half, g]
+            refs = b_vals[:, m, 2 * g : 2 * g + 2, :]
+            if g in SUMMED_IN_PSUM:
+                view = "p s (t h q) -> p s t h q"
+                nc.vector.tensor_tensor(
+                    parts[m, g][:].rearrange(view, t=PACK, h=2)[:, :, :, half, :],
+                    acc[:].rearrange("p s (q t) -> p s t q", t=PACK),
+                    refs.rearrange(view, t=PACK, h=2)[:, :, :, half, :],
+                    MULT,
                 )
-            nc.vector.tensor_tensor(
-                high_parts[j // 2][:, :, j % 2, :],
-                bank[:].rearrange("p (m c) -> p m c", m=2),
-                b_vals[:, :, j, HALF:],
-                MULT,
+            else:
+                cols = slice(half * HALF, (half + 1) * HALF)
+                nc.vector.tensor_tensor(parts[m, g][:, :, cols], acc[:], refs[:, :, cols], MULT)
+
+        sums = {}
+
+        def turn_part(m, g, s, n):
+            if m == 0:
+                sums[g, s] = bank(n, [P, PACK, TOK])
+            for t in range(PACK):
+                nc.tensor.matmul(
+                    sums[g, s][:, t, :], parts[m, g][:, s, t * P : (t + 1) * P], ident[:],
+                    start=(m == 0 and t == 0), stop=(m == 1 and t == PACK - 1), is_transpose=True,
+                )
+
+        h_bf = [sbuf(f"h_bf{g}", [P, 2, TOK * PACK], BF16) for g in range(PAIRS)]
+
+        def round_sum(copy, g, s):
+            copy(
+                out=h_bf[g][:, s, :].rearrange("p (r t) -> p r t", t=PACK),
+                in_=sums[g, s][:].rearrange("p t r -> p r t"),
             )
 
-        h_tok = [sbuf(f"h_tok{g}", [P, 2, H], BF16) for g in range(PAIRS)]
+        h_tok = {}
 
-        def add_parts(engine, real, imag, half, g, tiles):
-            engine.tensor_tensor(
-                h_tok[g][:, tiles, :].rearrange("p s (u h x) -> p s u h x", u=2, h=2)[:, :, :, half, :],
-                real[:, tiles, :].rearrange("p s (u x) -> p s u x", u=2),
-                imag[:, tiles, :].rearrange("p s (u x) -> p s u x", u=2),
+        def add_parts(g):
+            h_tok[g] = sbuf(f"h_tok{g}", [P, 2, 2, HALF], BF16)
+            view = "p s (q u e) -> p u (s q) e"
+            nc.vector.tensor_tensor(
+                h_tok[g][:].rearrange("p u s (q e) -> p u (s q) e", e=2),
+                parts[0, g][:].rearrange(view, u=2, e=2),
+                parts[1, g][:].rearrange(view, u=2, e=2),
                 ADD,
             )
 
-        def turn(g, tiles):
-            count = tiles.stop - tiles.start
-            xt = psum.tile([P, count, 2, TOK], F32, name="xt", tag="xt", bufs=2)
-            for s in range(count):
-                words = h_tok[g][:, tiles.start + s, :].bitcast(F32)
+        def turn_words(g, n):
+            xt = bank(n, [P, 2, 2, TOK])
+            for s in range(2):
                 for u in range(2):
-                    nc.tensor.transpose(xt[:, s, u, :], words[:, u * P : (u + 1) * P], ident[:])
-            grouped = sbuf(f"h_bf{g}{tiles.start}", [P, count * TOK * PACK], BF16)
+                    nc.tensor.transpose(xt[:, s, u, :], h_tok[g][:, u, s, :].bitcast(F32), ident[:])
             nc.scalar.copy(
-                out=grouped[:].bitcast(F32).rearrange("p (s r u) -> p s r u", s=count, u=2),
+                out=h_bf[g][:].bitcast(F32).rearrange("p s (r u) -> p s r u", u=2),
                 in_=xt[:].rearrange("p s u r -> p s r u"),
             )
-            return grouped
 
-        def beams(grouped, g, tiles, last):
+        def beams(g, tiles, banks, on_vector):
             width = (tiles.stop - tiles.start) * TOK
             first = g * PAIR + tiles.start * TOK
             codes = sbuf(f"h_codes{first}", [P, width], U32)
             scales = sbuf(f"h_scales{first}", [P, width], U8)
-            nc.vector.quantize_mx(out=codes[:].bitcast(FP8X4), scales=scales[:], in_=grouped[:])
+            nc.vector.quantize_mx(
+                out=codes[:].bitcast(FP8X4), scales=scales[:],
+                in_=h_bf[g][:, tiles, :].rearrange("p s x -> p (s x)"),
+            )
             result = sbuf(f"result{first}", [P, BEAM_TILES, width], F32)
             rows = out[:, first : first + width].rearrange("(c p) j -> p c j", p=P)
+            held = {n: bank(n, [P, banks.count(n), width]) for n in sorted(set(banks))}
+            ys = [held[n][:, banks[:c].count(n), :] for c, n in enumerate(banks)]
             for c in range(BEAM_TILES):
                 cols = slice(c * P, (c + 1) * P)
-                y = psum.tile([P, width], F32, name="y", tag="y", bufs=3)
                 nc.tensor.matmul_mx(
-                    out=y[:],
+                    out=ys[c],
                     lhsT=bm_words[:, cols].bitcast(FP8X4),
                     lhsT_scale=bm_scales[:].bitcast(U8)[:, cols],
                     rhs=codes[:].bitcast(FP8X4),
@@ -266,14 +281,15 @@ def tile_list_reference_matched_beams_kernel(
                     start=True,
                     stop=True,
                 )
-                if last and c == 1:
+            for c in range(BEAM_TILES):
+                if c in on_vector:
                     nc.vector.tensor_scalar(
-                        out=result[:, c, :], in0=y[:], scalar1=gain_cols[:, c : c + 1],
+                        out=result[:, c, :], in0=ys[c], scalar1=gain_cols[:, c : c + 1],
                         scalar2=base_cols[:, c : c + 1], op0=MULT, op1=ADD,
                     )
                 else:
                     nc.scalar.activation(
-                        out=result[:, c, :], in_=y[:], func=IDENTITY,
+                        out=result[:, c, :], in_=ys[c], func=IDENTITY,
                         bias=base_cols[:, c : c + 1], scale=gain_cols[:, c : c + 1],
                     )
             if first + width == S:
@@ -284,45 +300,62 @@ def tile_list_reference_matched_beams_kernel(
 
         reference_channels(0)
         reference_channels(1)
+        stage(0, 0, "stage_a")
+        stage(0, 1, "stage_b")
+        stage(1, 1, "stage_c")
         for a in range(PASSES):
             round_weights(nc.vector.tensor_copy, 0, 0, a)
-        for half, m, a in low[2:] + high:
-            round_weights(nc.scalar.copy, half, m, a)
+        for a in range(PASSES):
+            round_weights(nc.scalar.copy, 0, 1, a)
 
-        whole = [slice(0, PASSES)]
         both = slice(0, 2)
-        single = [slice(0, 1), slice(1, 2)]
-
-        weights = {(0, 0): quantize_weights(0, 0, whole)}
+        quantize_weights(0, 0)
+        for g in range(PAIRS):
+            accumulate(0, 0, g, g, [0])
         for first in (0, S // 2):
             gather(g_words[1], v_words[1][:].bitcast(U32), idx, first, first + S // 2)
 
-        real = [product(*weights[0, 0], 0, 0, g) for g in range(PAIRS - 1)]
-        weights[0, 1] = quantize_weights(0, 1, whole)
-        real.append(product(*weights[0, 0], 0, 0, PAIRS - 1))
-        imag = [product(*weights[0, 1], 0, 1, g) for g in range(2)]
-        quantize_high(0)
-        imag.append(product(*weights[0, 1], 0, 1, 2))
-        quantize_high(1)
-        imag.append(product(*weights[0, 1], 0, 1, 3))
-        for g in range(PAIRS):
-            for tiles in single:
-                add_parts(nc.gpsimd, real[g], imag[g], 0, g, tiles)
-
-        product_high(0)
-        product_high(1)
-        turned = {}
-        for g in range(PAIRS - 1):
-            product_high(2 * g + 2)
-            add_parts(nc.vector, high_parts[g][:, 0], high_parts[g][:, 1], 1, g, both)
-            turned[g] = turn(g, both)
-            product_high(2 * g + 3)
-            if g >= 1:
-                beams(turned[g - 1], g - 1, both, False)
-        ends = []
-        for tiles in single:
-            add_parts(nc.vector, high_parts[PAIRS - 1][:, 0], high_parts[PAIRS - 1][:, 1], 1, PAIRS - 1, tiles)
-            ends.append(turn(PAIRS - 1, tiles))
-        beams(turned[PAIRS - 2], PAIRS - 2, both, True)
-        for tiles, grouped in zip(single, ends):
-            beams(grouped, PAIRS - 1, tiles, True)
+        product(0, 0, 0, 0)
+        product(0, 0, 1, 1)
+        quantize_weights(0, 1)
+        parts[0, 2] = keep.tile([P, 2, H], F32, name="parts02", tag="stage_b", bufs=1, align_bytes=64)
+        stage(1, 0, "stage_d")
+        for a in range(PASSES):
+            round_weights(nc.scalar.copy, 1, 0, a)
+        for a in range(PASSES):
+            round_weights(nc.scalar.copy, 1, 1, a)
+        for g in range(2, PAIRS):
+            product(0, 0, g, g)
+        product(0, 1, 0, 0)
+        product(0, 1, 3, 1)
+        product(0, 1, 1, 2)
+        turn_part(0, 0, 0, 4)
+        turn_part(0, 0, 1, 5)
+        quantize_weights(1, 0)
+        product(0, 1, 2, 3)
+        product(1, 0, 0, 0)
+        turn_part(0, 3, 0, 6)
+        turn_part(0, 3, 1, 7)
+        product(1, 0, 1, 1)
+        quantize_weights(1, 1)
+        product(1, 0, 2, 2)
+        product(1, 1, 0, 3)
+        product(1, 1, 1, 0)
+        for s in range(2):
+            turn_part(1, 0, s, None)
+            round_sum(nc.scalar.copy, 0, s)
+        add_parts(1)
+        product(1, 1, 2, 1)
+        turn_words(1, 2)
+        beams(0, both, [4, 4, 5], [2])
+        product(1, 0, 3, 3)
+        add_parts(2)
+        product(1, 1, 3, 0)
+        turn_words(2, 1)
+        beams(1, both, [4, 4, 5], [])
+        for s in range(2):
+            turn_part(1, 3, s, None)
+            round_sum((nc.scalar.copy, nc.vector.tensor_copy)[s], 3, s)
+        beams(2, both, [2, 3, 0], [1])
+        beams(3, slice(0, 1), [4, 5, 6], [1])
+        beams(3, slice(1, 2), [1, 2, 7], [1])

@@ -29,7 +29,7 @@ PAIRS = S // PAIR
 HALF = H // 2
 BEAM_TILES = N // P
 SCALE_ROW = (4, 8)
-SUMMED_IN_PSUM = (0, 3)
+SUMMED_IN_PSUM = (0, 1)
 
 
 def tile_list_reference_matched_beams_kernel(
@@ -153,32 +153,40 @@ def tile_list_reference_matched_beams_kernel(
                         in_=acc[:].rearrange("p (q t) -> p t q", t=PACK),
                     )
                 else:
-                    nc.scalar.copy(out=b_vals[:, m, j, :], in_=acc[:])
+                    nc.scalar.copy(
+                        out=b_vals[:, m, j, :].rearrange("p (u q e) -> p u q e", u=2, e=2),
+                        in_=acc[:].rearrange("p (q u e) -> p u q e", u=2, e=2),
+                    )
 
-        wa_bf = {}
-
-        def stage(m, half, tag):
-            wa_bf[m, half] = keep.tile([P, PASSES, HALF, PACK], BF16, name=f"wa_bf{m}{half}", tag=tag, bufs=1, align_bytes=64)
+        wa_bf = {piece: sbuf(f"wa_bf{piece[0]}{piece[1]}", [P, PASSES, HALF, PACK], BF16) for piece in pieces}
 
         def round_weights(copy, m, half, a):
             copy(
-                out=wa_bf[m, half][:, a, :, :].rearrange("p (q t) j -> p q j t", t=PACK),
-                in_=wa_raw[m, half, a][:].rearrange("p j (q t) -> p q j t", t=PACK),
+                out=wa_bf[m, half][:, a, :, :].rearrange("p (u q e) j -> p q j u e", u=2, e=2),
+                in_=wa_raw[m, half, a][:].rearrange("p j (q u e) -> p q j u e", u=2, e=2),
             )
 
-        weights = {}
+        weights = {
+            (m, half): (sbuf(f"wa_codes{m}{half}", [P, PASSES, HALF], U32), sbuf(f"wa_scales{m}{half}", [P, PASSES, HALF], U8))
+            for m, half in pieces
+        }
 
-        def quantize_weights(m, half):
-            codes = sbuf(f"wa_codes{m}{half}", [P, PASSES, HALF], U32)
-            scales = sbuf(f"wa_scales{m}{half}", [P, PASSES, HALF], U8)
+        def quantize_weights(m, half, passes):
+            codes, scales = weights[m, half]
             nc.vector.quantize_mx(
-                out=codes[:].rearrange("p a c -> p (a c)").bitcast(FP8X4),
-                scales=scales[:].rearrange("p a c -> p (a c)"),
-                in_=wa_bf[m, half][:].rearrange("p a c j -> p (a c j)"),
+                out=codes[:, passes, :].rearrange("p a c -> p (a c)").bitcast(FP8X4),
+                scales=scales[:, passes, :].rearrange("p a c -> p (a c)"),
+                in_=wa_bf[m, half][:, passes].rearrange("p a c j -> p (a c j)"),
             )
-            weights[m, half] = codes, scales
 
-        parts = {(m, g): sbuf(f"parts{m}{g}", [P, 2, H], F32) for m in range(2) for g in range(PAIRS) if (m, g) != (0, 2)}
+        def after_rounding(m, half, shape):
+            return keep.tile(shape, F32, name=f"after{m}{half}", tag=f"wa_raw{m}{half}1", align_bytes=64)
+
+        parts = {(m, 0): sbuf(f"parts{m}0", [P, 2, H], F32) for m in range(2)}
+        parts[0, 1] = sbuf("parts01", [P, 2, H], F32)
+        for half in range(2):
+            for g in (2, 3):
+                parts[1, half, g] = sbuf(f"parts1{half}{g}", [P, 2, HALF], F32)[:]
 
         accs = {}
 
@@ -200,21 +208,29 @@ def tile_list_reference_matched_beams_kernel(
                         stop=(a == PASSES - 1 and s == 1),
                     )
 
-        def product(m, half, g, n):
-            accumulate(m, half, g, n, [1] if (m, half, g) in accs else [0, 1])
+        def multiply(m, half, g):
             acc = accs[m, half, g]
             refs = b_vals[:, m, 2 * g : 2 * g + 2, :]
             if g in SUMMED_IN_PSUM:
-                view = "p s (t h q) -> p s t h q"
+                view = "p s (u e h q) -> p (s u) e h q"
                 nc.vector.tensor_tensor(
-                    parts[m, g][:].rearrange(view, t=PACK, h=2)[:, :, :, half, :],
-                    acc[:].rearrange("p s (q t) -> p s t q", t=PACK),
-                    refs.rearrange(view, t=PACK, h=2)[:, :, :, half, :],
+                    parts[m, g][:].rearrange(view, u=2, e=2, h=2)[:, :, :, half, :],
+                    acc[:].rearrange("p s (u q e) -> p (s u) e q", u=2, e=2),
+                    refs.rearrange(view, u=2, e=2, h=2)[:, :, :, half, :],
                     MULT,
                 )
             else:
-                cols = slice(half * HALF, (half + 1) * HALF)
-                nc.vector.tensor_tensor(parts[m, g][:, :, cols], acc[:], refs[:, :, cols], MULT)
+                view = "p s (u h x) -> p (s u) h x"
+                nc.vector.tensor_tensor(
+                    parts[m, half, g].rearrange("p s (u x) -> p (s u) x", u=2),
+                    acc[:].rearrange("p s (u x) -> p (s u) x", u=2),
+                    refs.rearrange(view, u=2, h=2)[:, :, half, :],
+                    MULT,
+                )
+
+        def product(m, half, g, n):
+            accumulate(m, half, g, n, [1] if (m, half, g) in accs else [0, 1])
+            multiply(m, half, g)
 
         sums = {}
 
@@ -235,25 +251,25 @@ def tile_list_reference_matched_beams_kernel(
                 in_=sums[g, s][:].rearrange("p t r -> p r t"),
             )
 
-        h_tok = {}
+        h_tok = [sbuf(f"h_tok{g}", [P, 2, H], BF16) for g in range(PAIRS)]
 
-        def add_parts(g):
-            h_tok[g] = sbuf(f"h_tok{g}", [P, 2, 2, HALF], BF16)
-            view = "p s (q u e) -> p u (s q) e"
+        def add_parts(g, tiles, half):
             nc.vector.tensor_tensor(
-                h_tok[g][:].rearrange("p u s (q e) -> p u (s q) e", e=2),
-                parts[0, g][:].rearrange(view, u=2, e=2),
-                parts[1, g][:].rearrange(view, u=2, e=2),
+                h_tok[g][:, tiles, :].rearrange("p s (u h x) -> p s u h x", u=2, h=2)[:, :, :, half, :],
+                parts[0, half, g][:, tiles, :].rearrange("p s (u x) -> p s u x", u=2),
+                parts[1, half, g][:, tiles, :].rearrange("p s (u x) -> p s u x", u=2),
                 ADD,
             )
 
-        def turn_words(g, n):
-            xt = bank(n, [P, 2, 2, TOK])
-            for s in range(2):
+        def turn_words(g, tiles, n):
+            count = tiles.stop - tiles.start
+            xt = bank(n, [P, count, 2, TOK])
+            for s in range(count):
+                words = h_tok[g][:, tiles.start + s, :].bitcast(F32)
                 for u in range(2):
-                    nc.tensor.transpose(xt[:, s, u, :], h_tok[g][:, u, s, :].bitcast(F32), ident[:])
+                    nc.tensor.transpose(xt[:, s, u, :], words[:, u * P : (u + 1) * P], ident[:])
             nc.scalar.copy(
-                out=h_bf[g][:].bitcast(F32).rearrange("p s (r u) -> p s r u", u=2),
+                out=h_bf[g][:, tiles, :].bitcast(F32).rearrange("p s (r u) -> p s r u", u=2),
                 in_=xt[:].rearrange("p s u r -> p s r u"),
             )
 
@@ -300,16 +316,14 @@ def tile_list_reference_matched_beams_kernel(
 
         reference_channels(0)
         reference_channels(1)
-        stage(0, 0, "stage_a")
-        stage(0, 1, "stage_b")
-        stage(1, 1, "stage_c")
         for a in range(PASSES):
             round_weights(nc.vector.tensor_copy, 0, 0, a)
-        for a in range(PASSES):
-            round_weights(nc.scalar.copy, 0, 1, a)
+        for m, half in pieces[1:]:
+            for a in range(PASSES):
+                round_weights(nc.scalar.copy, m, half, a)
 
         both = slice(0, 2)
-        quantize_weights(0, 0)
+        quantize_weights(0, 0, both)
         for g in range(PAIRS):
             accumulate(0, 0, g, g, [0])
         for first in (0, S // 2):
@@ -317,45 +331,52 @@ def tile_list_reference_matched_beams_kernel(
 
         product(0, 0, 0, 0)
         product(0, 0, 1, 1)
-        quantize_weights(0, 1)
-        parts[0, 2] = keep.tile([P, 2, H], F32, name="parts02", tag="stage_b", bufs=1, align_bytes=64)
-        stage(1, 0, "stage_d")
-        for a in range(PASSES):
-            round_weights(nc.scalar.copy, 1, 0, a)
-        for a in range(PASSES):
-            round_weights(nc.scalar.copy, 1, 1, a)
-        for g in range(2, PAIRS):
+        quantize_weights(0, 1, both)
+        held = after_rounding(0, 1, [P, 2, 2, HALF])
+        for g in (2, 3):
+            parts[0, 0, g] = held[:, g - 2]
             product(0, 0, g, g)
         product(0, 1, 0, 0)
-        product(0, 1, 3, 1)
-        product(0, 1, 1, 2)
+        product(0, 1, 1, 1)
         turn_part(0, 0, 0, 4)
         turn_part(0, 0, 1, 5)
-        quantize_weights(1, 0)
-        product(0, 1, 2, 3)
+        quantize_weights(1, 0, both)
+        held = after_rounding(1, 0, [P, 2, 2, HALF])
+        for g in (2, 3):
+            parts[0, 1, g] = held[:, g - 2]
+            product(0, 1, g, g)
         product(1, 0, 0, 0)
-        turn_part(0, 3, 0, 6)
-        turn_part(0, 3, 1, 7)
-        product(1, 0, 1, 1)
-        quantize_weights(1, 1)
-        product(1, 0, 2, 2)
-        product(1, 1, 0, 3)
-        product(1, 1, 1, 0)
+        accumulate(1, 0, 1, 1, [0, 1])
+        turn_part(0, 1, 0, 6)
+        turn_part(0, 1, 1, 7)
+        for a in range(PASSES):
+            quantize_weights(1, 1, slice(a, a + 1))
+        parts[1, 1] = after_rounding(1, 1, [P, 2, H])
+        multiply(1, 0, 1)
+        product(1, 1, 0, 2)
+        product(1, 1, 1, 3)
+        accumulate(1, 1, 2, 0, [0, 1])
         for s in range(2):
             turn_part(1, 0, s, None)
             round_sum(nc.scalar.copy, 0, s)
-        add_parts(1)
-        product(1, 1, 2, 1)
-        turn_words(1, 2)
-        beams(0, both, [4, 4, 5], [2])
-        product(1, 0, 3, 3)
-        add_parts(2)
-        product(1, 1, 3, 0)
-        turn_words(2, 1)
-        beams(1, both, [4, 4, 5], [])
+        multiply(1, 1, 2)
+        product(1, 0, 2, 1)
         for s in range(2):
-            turn_part(1, 3, s, None)
-            round_sum((nc.scalar.copy, nc.vector.tensor_copy)[s], 3, s)
-        beams(2, both, [2, 3, 0], [1])
-        beams(3, slice(0, 1), [4, 5, 6], [1])
-        beams(3, slice(1, 2), [1, 2, 7], [1])
+            turn_part(1, 1, s, None)
+            round_sum(nc.scalar.copy, 1, s)
+        accumulate(1, 0, 3, 2, [0, 1])
+        add_parts(2, both, 1)
+        beams(0, both, [4, 4, 5], [])
+        add_parts(2, both, 0)
+        accumulate(1, 1, 3, 3, [0, 1])
+        multiply(1, 0, 3)
+        turn_words(2, both, 0)
+        beams(1, both, [6, 6, 7], [])
+        add_parts(3, both, 0)
+        multiply(1, 1, 3)
+        for s in range(2):
+            add_parts(3, slice(s, s + 1), 1)
+            turn_words(3, slice(s, s + 1), 1 + s)
+        beams(2, both, [4, 5, 0], [1])
+        beams(3, slice(0, 1), [3, 6, 7], [1])
+        beams(3, slice(1, 2), [1, 2, 5], [1])

@@ -179,11 +179,10 @@ def tile_list_reference_matched_beams_kernel(
                 in_=wa_bf[m, half][:, passes].rearrange("p a c j -> p (a c j)"),
             )
 
-        def after_rounding(m, half, shape):
-            return keep.tile(shape, F32, name=f"after{m}{half}", tag=f"wa_raw{m}{half}1", align_bytes=64)
+        def after_rounding(m, half, a, shape):
+            return keep.tile(shape, F32, name=f"after{m}{half}{a}", tag=f"wa_raw{m}{half}{a}", align_bytes=64)
 
         parts = {(m, 0): sbuf(f"parts{m}0", [P, 2, H], F32) for m in range(2)}
-        parts[0, 1] = sbuf("parts01", [P, 2, H], F32)
         for half in range(2):
             for g in (2, 3):
                 parts[1, half, g] = sbuf(f"parts1{half}{g}", [P, 2, HALF], F32)[:]
@@ -253,22 +252,22 @@ def tile_list_reference_matched_beams_kernel(
 
         h_tok = [sbuf(f"h_tok{g}", [P, 2, H], BF16) for g in range(PAIRS)]
 
-        def add_parts(g, tiles, half):
-            nc.vector.tensor_tensor(
+        def add_parts(engine, g, tiles, half):
+            engine.tensor_tensor(
                 h_tok[g][:, tiles, :].rearrange("p s (u h x) -> p s u h x", u=2, h=2)[:, :, :, half, :],
                 parts[0, half, g][:, tiles, :].rearrange("p s (u x) -> p s u x", u=2),
                 parts[1, half, g][:, tiles, :].rearrange("p s (u x) -> p s u x", u=2),
                 ADD,
             )
 
-        def turn_words(g, tiles, n):
+        def turn_words(copy, g, tiles, n):
             count = tiles.stop - tiles.start
             xt = bank(n, [P, count, 2, TOK])
             for s in range(count):
                 words = h_tok[g][:, tiles.start + s, :].bitcast(F32)
                 for u in range(2):
                     nc.tensor.transpose(xt[:, s, u, :], words[:, u * P : (u + 1) * P], ident[:])
-            nc.scalar.copy(
+            copy(
                 out=h_bf[g][:, tiles, :].bitcast(F32).rearrange("p s (r u) -> p s r u", u=2),
                 in_=xt[:].rearrange("p s u r -> p s r u"),
             )
@@ -308,10 +307,12 @@ def tile_list_reference_matched_beams_kernel(
                         out=result[:, c, :], in_=ys[c], func=IDENTITY,
                         bias=base_cols[:, c : c + 1], scale=gain_cols[:, c : c + 1],
                     )
+                if g == PAIRS - 2:
+                    nc.sync.dma_start(out=rows[:, c, :], in_=result[:, c, :])
             if first + width == S:
                 nc.sync.dma_start(out=rows[:, :2, :], in_=result[:, :2, :])
                 nc.scalar.dma_start(out=rows[:, 2, :], in_=result[:, 2, :])
-            else:
+            elif g != PAIRS - 2:
                 nc.sync.dma_start(out=rows, in_=result[:])
 
         reference_channels(0)
@@ -329,54 +330,62 @@ def tile_list_reference_matched_beams_kernel(
         for first in (0, S // 2):
             gather(g_words[1], v_words[1][:].bitcast(U32), idx, first, first + S // 2)
 
-        product(0, 0, 0, 0)
-        product(0, 0, 1, 1)
-        quantize_weights(0, 1, both)
-        held = after_rounding(0, 1, [P, 2, 2, HALF])
+        for g in range(PAIRS):
+            accumulate(0, 0, g, g, [1])
+        multiply(0, 0, 0)
+        quantize_weights(0, 1, slice(0, 1))
+        for g in range(PAIRS):
+            accumulate(0, 1, g, 4 + g, [0])
+        parts[0, 1] = after_rounding(0, 1, 0, [P, 2, H])
+        multiply(0, 0, 1)
+        quantize_weights(0, 1, slice(1, 2))
+        for g in range(PAIRS):
+            accumulate(0, 1, g, 4 + g, [1])
+        held = after_rounding(0, 1, 1, [P, 2, 2, HALF])
         for g in (2, 3):
             parts[0, 0, g] = held[:, g - 2]
-            product(0, 0, g, g)
-        product(0, 1, 0, 0)
-        product(0, 1, 1, 1)
-        turn_part(0, 0, 0, 4)
-        turn_part(0, 0, 1, 5)
+            multiply(0, 0, g)
+        multiply(0, 1, 0)
+        multiply(0, 1, 1)
+        turn_part(0, 0, 0, 0)
+        turn_part(0, 0, 1, 1)
         quantize_weights(1, 0, both)
-        held = after_rounding(1, 0, [P, 2, 2, HALF])
+        held = after_rounding(1, 0, 1, [P, 2, 2, HALF])
         for g in (2, 3):
             parts[0, 1, g] = held[:, g - 2]
-            product(0, 1, g, g)
-        product(1, 0, 0, 0)
-        accumulate(1, 0, 1, 1, [0, 1])
-        turn_part(0, 1, 0, 6)
-        turn_part(0, 1, 1, 7)
+            multiply(0, 1, g)
+        product(1, 0, 0, 2)
+        accumulate(1, 0, 1, 3, [0, 1])
+        turn_part(0, 1, 0, 4)
+        turn_part(0, 1, 1, 5)
         for a in range(PASSES):
             quantize_weights(1, 1, slice(a, a + 1))
-        parts[1, 1] = after_rounding(1, 1, [P, 2, H])
+        parts[1, 1] = after_rounding(1, 1, 1, [P, 2, H])
         multiply(1, 0, 1)
-        product(1, 1, 0, 2)
-        product(1, 1, 1, 3)
-        accumulate(1, 1, 2, 0, [0, 1])
+        product(1, 1, 0, 6)
+        product(1, 1, 1, 7)
+        accumulate(1, 1, 2, 2, [0, 1])
         for s in range(2):
             turn_part(1, 0, s, None)
             round_sum(nc.scalar.copy, 0, s)
         multiply(1, 1, 2)
-        product(1, 0, 2, 1)
+        product(1, 0, 2, 3)
         for s in range(2):
             turn_part(1, 1, s, None)
             round_sum(nc.scalar.copy, 1, s)
-        accumulate(1, 0, 3, 2, [0, 1])
-        add_parts(2, both, 1)
-        beams(0, both, [4, 4, 5], [])
-        add_parts(2, both, 0)
-        accumulate(1, 1, 3, 3, [0, 1])
+        accumulate(1, 0, 3, 6, [0, 1])
+        add_parts(nc.vector, 2, both, 1)
+        beams(0, both, [0, 0, 1], [])
+        add_parts(nc.vector, 2, both, 0)
+        accumulate(1, 1, 3, 7, [0, 1])
         multiply(1, 0, 3)
-        turn_words(2, both, 0)
-        beams(1, both, [6, 6, 7], [])
-        add_parts(3, both, 0)
+        turn_words(nc.scalar.copy, 2, both, 2)
+        beams(1, both, [4, 4, 5], [])
+        add_parts(nc.vector, 3, both, 0)
         multiply(1, 1, 3)
         for s in range(2):
-            add_parts(3, slice(s, s + 1), 1)
-            turn_words(3, slice(s, s + 1), 1 + s)
-        beams(2, both, [4, 5, 0], [1])
-        beams(3, slice(0, 1), [3, 6, 7], [1])
-        beams(3, slice(1, 2), [1, 2, 5], [1])
+            add_parts(nc.vector, 3, slice(s, s + 1), 1)
+            turn_words((nc.scalar.copy, nc.vector.tensor_copy)[s], 3, slice(s, s + 1), (3, 6)[s])
+        beams(2, both, [0, 1, 2], [1])
+        beams(3, slice(0, 1), [7, 4, 5], [1])
+        beams(3, slice(1, 2), [3, 6, 1], [1])

@@ -29,7 +29,12 @@ PAIRS = S // PAIR
 HALF = H // 2
 BEAM_TILES = N // P
 SCALE_ROW = (4, 8)
+REAL, IMAG = 0, 1
+LOW, HIGH = 0, 1
+PIECES = ((REAL, LOW), (REAL, HIGH), (IMAG, LOW), (IMAG, HIGH))
 SUMMED_IN_PSUM = (0, 1)
+ADDED_ON_VECTOR = (2, 3)
+REFERENCE_BANKS = (5, 6, 7)
 
 
 def tile_list_reference_matched_beams_kernel(
@@ -52,8 +57,8 @@ def tile_list_reference_matched_beams_kernel(
         v_scales = sbuf("v_scales", [P, T // 4], I32)
         v2_words = sbuf("v2_words", [P, T2], I32)
         v2_scales = sbuf("v2_scales", [P, T2 // 4], I32)
-        wb_words = [sbuf(f"wb_words{m}", [P, 2 * H // 4], I32) for m in range(2)]
-        wb_scales = [sbuf(f"wb_scales{m}", [P, H // 4], I32) for m in range(2)]
+        wb_words = [sbuf(f"wb_words{m}", [P, 2 * H // 4], I32) for m in (REAL, IMAG)]
+        wb_scales = [sbuf(f"wb_scales{m}", [P, H // 4], I32) for m in (REAL, IMAG)]
         bm_words = sbuf("bm_words", [P, N], I32)
         bm_scales = sbuf("bm_scales", [P, N // 4], I32)
         gain_cols = sbuf("gain_cols", [P, BEAM_TILES], F32)
@@ -62,19 +67,13 @@ def tile_list_reference_matched_beams_kernel(
 
         nc.gpsimd.memset(v2_scales[:], 0)
         nc.vector.memset(v_scales[:], 0)
-        nc.vector.memset(wb_scales[0][:], 0)
-        nc.vector.memset(wb_scales[1][:], 0)
+        nc.vector.memset(wb_scales[REAL][:], 0)
+        nc.vector.memset(wb_scales[IMAG][:], 0)
         nc.vector.memset(bm_scales[:], 0)
 
-        def load_scale_rows(plane, rows):
+        def load_scale_rows(scale_tile, rows):
             for r in range(4):
-                nc.sync.dma_start(out=plane[r:P:32, :], in_=rows[0, r:16:4, :].bitcast(I32))
-
-        def load_table_scales(queue, q):
-            queue.dma_start(
-                out=v_scales[32 * q + 4 : 32 * q + 12, :],
-                in_=tab_scales[:, 4 * q : 4 * q + 4, :].bitcast(I32),
-            )
+                nc.sync.dma_start(out=scale_tile[r:P:32, :], in_=rows[0, r:16:4, :].bitcast(I32))
 
         def words_of(dram, a):
             return dram[a].rearrange("p t i -> p (t i)").bitcast(I32)
@@ -84,23 +83,25 @@ def tile_list_reference_matched_beams_kernel(
             nc.sync.dma_start(out=v_words[a][:, cols], in_=words_of(tab_words, a)[:, cols])
 
         nc.sync.dma_start(idx2[:], offs2)
-        nc.sync.dma_start(out=wb_words[0][:], in_=wbr_words[0].bitcast(I32))
+        nc.sync.dma_start(out=wb_words[REAL][:], in_=wbr_words[0].bitcast(I32))
         nc.sync.dma_start(out=v2_words[:, : T2 // 2], in_=words_of(tab2_words, 0)[:, : T2 // 2])
         load_scale_rows(v2_scales, tab2_scales)
         nc.sync.dma_start(out=v2_words[:, T2 // 2 :], in_=words_of(tab2_words, 0)[:, T2 // 2 :])
         load_table(0, 0, T // 4)
-        load_scale_rows(wb_scales[0], wbr_scales)
-        for q in range(4):
-            load_table_scales(nc.gpsimd, q)
+        load_scale_rows(wb_scales[REAL], wbr_scales)
+        for quadrant in range(4):
+            nc.gpsimd.dma_start(
+                out=v_scales[32 * quadrant + SCALE_ROW[0] : 32 * quadrant + SCALE_ROW[1] + 4, :],
+                in_=tab_scales[:, 4 * quadrant : 4 * quadrant + 4, :].bitcast(I32),
+            )
         nc.sync.dma_start(idx[:], offs)
         load_table(0, T // 4, T)
-        nc.sync.dma_start(out=wb_words[1][:], in_=wbi_words[0].bitcast(I32))
-        load_scale_rows(wb_scales[1], wbi_scales)
+        nc.sync.dma_start(out=wb_words[IMAG][:], in_=wbi_words[0].bitcast(I32))
+        load_scale_rows(wb_scales[IMAG], wbi_scales)
 
         wa_raw = {}
-        pieces = [(0, 0), (0, 1), (1, 0), (1, 1)]
-        for m, half in pieces:
-            if (m, half) == (0, 1):
+        for m, half in PIECES:
+            if (m, half) == PIECES[1]:
                 load_table(1, 0, T // 2)
                 load_table(1, T // 2, T)
             for a in range(PASSES):
@@ -124,7 +125,7 @@ def tile_list_reference_matched_beams_kernel(
         g2_scales = sbuf("g2_scales", [P, S], U8)
 
         gather(g2_scales, v2_scales[:].bitcast(U8), idx2, 0, S)
-        for first, last in ((0, 256), (256, 512), (512, S)):
+        for first, last in ((0, PAIR), (PAIR, 2 * PAIR), (2 * PAIR, S)):
             gather(g2_words, v2_words[:].bitcast(U32), idx2, first, last)
         gather(g_words[0], v_words[0][:].bitcast(U32), idx, 0, S)
         gather(g_scales, v_scales[:].bitcast(U8), idx, 0, S)
@@ -137,7 +138,7 @@ def tile_list_reference_matched_beams_kernel(
         def reference_channels(m):
             for j in range(TILES):
                 tok = slice(j * TOK, (j + 1) * TOK)
-                acc = bank(5 + (m * TILES + j) % 3, [P, H])
+                acc = bank(REFERENCE_BANKS[(m * TILES + j) % len(REFERENCE_BANKS)], [P, H])
                 nc.tensor.matmul_mx(
                     out=acc[:],
                     lhsT=g2_words[:, tok].bitcast(FP8X4),
@@ -149,56 +150,60 @@ def tile_list_reference_matched_beams_kernel(
                 )
                 if j // 2 in SUMMED_IN_PSUM:
                     nc.scalar.copy(
-                        out=b_vals[:, m, j, :].rearrange("p (t q) -> p t q", t=PACK),
-                        in_=acc[:].rearrange("p (q t) -> p t q", t=PACK),
+                        out=b_vals[:, m, j, :].rearrange("x (t p) -> x t p", t=PACK),
+                        in_=acc[:].rearrange("x (p t) -> x t p", t=PACK),
                     )
                 else:
                     nc.scalar.copy(
-                        out=b_vals[:, m, j, :].rearrange("p (u q e) -> p u q e", u=2, e=2),
-                        in_=acc[:].rearrange("p (q u e) -> p u q e", u=2, e=2),
+                        out=b_vals[:, m, j, :].rearrange("x (u p e) -> x u p e", u=2, e=2),
+                        in_=acc[:].rearrange("x (p u e) -> x u p e", u=2, e=2),
                     )
 
-        wa_bf = {piece: sbuf(f"wa_bf{piece[0]}{piece[1]}", [P, PASSES, HALF, PACK], BF16) for piece in pieces}
+        wa_bf = {(m, half): sbuf(f"wa_bf{m}{half}", [P, PASSES, HALF, PACK], BF16) for m, half in PIECES}
 
         def round_weights(copy, m, half, a):
             copy(
-                out=wa_bf[m, half][:, a, :, :].rearrange("p (u q e) j -> p q j u e", u=2, e=2),
-                in_=wa_raw[m, half, a][:].rearrange("p j (q u e) -> p q j u e", u=2, e=2),
+                out=wa_bf[m, half][:, a, :, :].rearrange("x (u q e) j -> x q j u e", u=2, e=2),
+                in_=wa_raw[m, half, a][:].rearrange("x j (q u e) -> x q j u e", u=2, e=2),
             )
 
         weights = {
-            (m, half): (sbuf(f"wa_codes{m}{half}", [P, PASSES, HALF], U32), sbuf(f"wa_scales{m}{half}", [P, PASSES, HALF], U8))
-            for m, half in pieces
+            (m, half): (
+                sbuf(f"wa_codes{m}{half}", [P, PASSES, HALF], U32),
+                sbuf(f"wa_scales{m}{half}", [P, PASSES, HALF], U8),
+            )
+            for m, half in PIECES
         }
 
         def quantize_weights(m, half, passes):
             codes, scales = weights[m, half]
+            span = slice(passes[0], passes[-1] + 1)
             nc.vector.quantize_mx(
-                out=codes[:, passes, :].rearrange("p a c -> p (a c)").bitcast(FP8X4),
-                scales=scales[:, passes, :].rearrange("p a c -> p (a c)"),
-                in_=wa_bf[m, half][:, passes].rearrange("p a c j -> p (a c j)"),
+                out=codes[:, span, :].rearrange("x a c -> x (a c)").bitcast(FP8X4),
+                scales=scales[:, span, :].rearrange("x a c -> x (a c)"),
+                in_=wa_bf[m, half][:, span].rearrange("x a c j -> x (a c j)"),
             )
 
         def after_rounding(m, half, a, shape):
             return keep.tile(shape, F32, name=f"after{m}{half}{a}", tag=f"wa_raw{m}{half}{a}", align_bytes=64)
 
-        parts = {(m, 0): sbuf(f"parts{m}0", [P, 2, H], F32) for m in range(2)}
-        for half in range(2):
-            for g in (2, 3):
-                parts[1, half, g] = sbuf(f"parts1{half}{g}", [P, 2, HALF], F32)[:]
+        rows_of = {(m, 0): sbuf(f"rows_of{m}0", [P, 2, H], F32) for m in (REAL, IMAG)}
+        halves_of = {}
+        for half in (LOW, HIGH):
+            for g in ADDED_ON_VECTOR:
+                halves_of[IMAG, half, g] = sbuf(f"halves_of1{half}{g}", [P, 2, HALF], F32)[:]
 
         accs = {}
 
-        def accumulate(m, half, g, n, passes):
+        def accumulate(m, half, g, passes, n=None):
             codes, scales = weights[m, half]
             if 0 in passes:
                 accs[m, half, g] = bank(n, [P, 2, HALF])
-            acc = accs[m, half, g]
             for a in passes:
                 for s in range(2):
                     tok = slice(g * PAIR + s * TOK, g * PAIR + (s + 1) * TOK)
                     nc.tensor.matmul_mx(
-                        out=acc[:, s, :],
+                        out=accs[m, half, g][:, s, :],
                         lhsT=g_words[a][:, tok].bitcast(FP8X4),
                         lhsT_scale=g_scales[SCALE_ROW[a] :, tok],
                         rhs=codes[:, a, :].bitcast(FP8X4),
@@ -211,66 +216,69 @@ def tile_list_reference_matched_beams_kernel(
             acc = accs[m, half, g]
             refs = b_vals[:, m, 2 * g : 2 * g + 2, :]
             if g in SUMMED_IN_PSUM:
-                view = "p s (u e h q) -> p (s u) e h q"
+                view = "x s (u e h q) -> x (s u) e h q"
                 nc.vector.tensor_tensor(
-                    parts[m, g][:].rearrange(view, u=2, e=2, h=2)[:, :, :, half, :],
-                    acc[:].rearrange("p s (u q e) -> p (s u) e q", u=2, e=2),
+                    rows_of[m, g][:].rearrange(view, u=2, e=2, h=2)[:, :, :, half, :],
+                    acc[:].rearrange("x s (u q e) -> x (s u) e q", u=2, e=2),
                     refs.rearrange(view, u=2, e=2, h=2)[:, :, :, half, :],
                     MULT,
                 )
             else:
-                view = "p s (u h x) -> p (s u) h x"
                 nc.vector.tensor_tensor(
-                    parts[m, half, g].rearrange("p s (u x) -> p (s u) x", u=2),
-                    acc[:].rearrange("p s (u x) -> p (s u) x", u=2),
-                    refs.rearrange(view, u=2, h=2)[:, :, half, :],
+                    halves_of[m, half, g].rearrange("x s (u c) -> x (s u) c", u=2),
+                    acc[:].rearrange("x s (u c) -> x (s u) c", u=2),
+                    refs.rearrange("x s (u h c) -> x (s u) h c", u=2, h=2)[:, :, half, :],
                     MULT,
                 )
 
         def product(m, half, g, n):
-            accumulate(m, half, g, n, [1] if (m, half, g) in accs else [0, 1])
+            accumulate(m, half, g, [0, 1], n)
             multiply(m, half, g)
 
         sums = {}
 
-        def turn_part(m, g, s, n):
-            if m == 0:
+        def turn_product(m, g, s, n=None):
+            if m == REAL:
                 sums[g, s] = bank(n, [P, PACK, TOK])
             for t in range(PACK):
                 nc.tensor.matmul(
-                    sums[g, s][:, t, :], parts[m, g][:, s, t * P : (t + 1) * P], ident[:],
-                    start=(m == 0 and t == 0), stop=(m == 1 and t == PACK - 1), is_transpose=True,
+                    sums[g, s][:, t, :], rows_of[m, g][:, s, t * P : (t + 1) * P], ident[:],
+                    start=(m == REAL and t == 0), stop=(m == IMAG and t == PACK - 1), is_transpose=True,
                 )
 
         h_bf = [sbuf(f"h_bf{g}", [P, 2, TOK * PACK], BF16) for g in range(PAIRS)]
 
-        def round_sum(copy, g, s):
-            copy(
-                out=h_bf[g][:, s, :].rearrange("p (r t) -> p r t", t=PACK),
-                in_=sums[g, s][:].rearrange("p t r -> p r t"),
-            )
+        def finish_sums(g):
+            for s in range(2):
+                turn_product(IMAG, g, s)
+                nc.scalar.copy(
+                    out=h_bf[g][:, s, :].rearrange("p (j t) -> p j t", t=PACK),
+                    in_=sums[g, s][:].rearrange("p t j -> p j t"),
+                )
 
-        h_tok = [sbuf(f"h_tok{g}", [P, 2, H], BF16) for g in range(PAIRS)]
+        h_tok = {g: sbuf(f"h_tok{g}", [P, 2, H], BF16) for g in ADDED_ON_VECTOR}
 
-        def add_parts(engine, g, tiles, half):
-            engine.tensor_tensor(
-                h_tok[g][:, tiles, :].rearrange("p s (u h x) -> p s u h x", u=2, h=2)[:, :, :, half, :],
-                parts[0, half, g][:, tiles, :].rearrange("p s (u x) -> p s u x", u=2),
-                parts[1, half, g][:, tiles, :].rearrange("p s (u x) -> p s u x", u=2),
+        def add_halves(g, tiles, half):
+            nc.vector.tensor_tensor(
+                h_tok[g][:, tiles, :].rearrange("x s (u h c) -> x s u h c", u=2, h=2)[:, :, :, half, :],
+                halves_of[REAL, half, g][:, tiles, :].rearrange("x s (u c) -> x s u c", u=2),
+                halves_of[IMAG, half, g][:, tiles, :].rearrange("x s (u c) -> x s u c", u=2),
                 ADD,
             )
 
         def turn_words(copy, g, tiles, n):
             count = tiles.stop - tiles.start
-            xt = bank(n, [P, count, 2, TOK])
+            turned = bank(n, [P, count, 2, TOK])
             for s in range(count):
                 words = h_tok[g][:, tiles.start + s, :].bitcast(F32)
                 for u in range(2):
-                    nc.tensor.transpose(xt[:, s, u, :], words[:, u * P : (u + 1) * P], ident[:])
+                    nc.tensor.transpose(turned[:, s, u, :], words[:, u * P : (u + 1) * P], ident[:])
             copy(
-                out=h_bf[g][:, tiles, :].bitcast(F32).rearrange("p s (r u) -> p s r u", u=2),
-                in_=xt[:].rearrange("p s u r -> p s r u"),
+                out=h_bf[g][:, tiles, :].bitcast(F32).rearrange("p s (j u) -> p s j u", u=2),
+                in_=turned[:].rearrange("p s u j -> p s j u"),
             )
+
+        results = [sbuf(f"result{g}", [P, BEAM_TILES, PAIR], F32) for g in range(PAIRS)]
 
         def beams(g, tiles, banks, on_vector):
             width = (tiles.stop - tiles.start) * TOK
@@ -279,12 +287,12 @@ def tile_list_reference_matched_beams_kernel(
             scales = sbuf(f"h_scales{first}", [P, width], U8)
             nc.vector.quantize_mx(
                 out=codes[:].bitcast(FP8X4), scales=scales[:],
-                in_=h_bf[g][:, tiles, :].rearrange("p s x -> p (s x)"),
+                in_=h_bf[g][:, tiles, :].rearrange("p s c -> p (s c)"),
             )
-            result = sbuf(f"result{first}", [P, BEAM_TILES, width], F32)
-            rows = out[:, first : first + width].rearrange("(c p) j -> p c j", p=P)
-            held = {n: bank(n, [P, banks.count(n), width]) for n in sorted(set(banks))}
-            ys = [held[n][:, banks[:c].count(n), :] for c, n in enumerate(banks)]
+            result = results[g][:, :, tiles.start * TOK : tiles.stop * TOK]
+            rows = out[:, g * PAIR : (g + 1) * PAIR].rearrange("(c p) j -> p c j", p=P)
+            in_bank = {n: bank(n, [P, banks.count(n), width]) for n in sorted(set(banks))}
+            ys = [in_bank[n][:, banks[:c].count(n), :] for c, n in enumerate(banks)]
             for c in range(BEAM_TILES):
                 cols = slice(c * P, (c + 1) * P)
                 nc.tensor.matmul_mx(
@@ -296,6 +304,7 @@ def tile_list_reference_matched_beams_kernel(
                     start=True,
                     stop=True,
                 )
+            stored_by_tile = g >= PAIRS - 2
             for c in range(BEAM_TILES):
                 if c in on_vector:
                     nc.vector.tensor_scalar(
@@ -307,85 +316,87 @@ def tile_list_reference_matched_beams_kernel(
                         out=result[:, c, :], in_=ys[c], func=IDENTITY,
                         bias=base_cols[:, c : c + 1], scale=gain_cols[:, c : c + 1],
                     )
-                if g == PAIRS - 2:
-                    nc.sync.dma_start(out=rows[:, c, :], in_=result[:, c, :])
-            if first + width == S:
-                nc.sync.dma_start(out=rows[:, :2, :], in_=result[:, :2, :])
-                nc.scalar.dma_start(out=rows[:, 2, :], in_=result[:, 2, :])
-            elif g != PAIRS - 2:
+                if stored_by_tile and tiles.stop == 2:
+                    queue = nc.scalar if (g, c) == (PAIRS - 1, BEAM_TILES - 1) else nc.sync
+                    queue.dma_start(out=rows[:, c, :], in_=results[g][:, c, :])
+            if not stored_by_tile:
                 nc.sync.dma_start(out=rows, in_=result[:])
 
-        reference_channels(0)
-        reference_channels(1)
+        reference_channels(REAL)
+        reference_channels(IMAG)
         for a in range(PASSES):
-            round_weights(nc.vector.tensor_copy, 0, 0, a)
-        for m, half in pieces[1:]:
+            round_weights(nc.vector.tensor_copy, REAL, LOW, a)
+        for m, half in PIECES[1:]:
             for a in range(PASSES):
                 round_weights(nc.scalar.copy, m, half, a)
 
         both = slice(0, 2)
-        quantize_weights(0, 0, both)
+
+        quantize_weights(REAL, LOW, [0, 1])
         for g in range(PAIRS):
-            accumulate(0, 0, g, g, [0])
+            accumulate(REAL, LOW, g, [0], g)
         for first in (0, S // 2):
             gather(g_words[1], v_words[1][:].bitcast(U32), idx, first, first + S // 2)
+        for g in range(PAIRS):
+            accumulate(REAL, LOW, g, [1])
 
+        multiply(REAL, LOW, 0)
+        quantize_weights(REAL, HIGH, [0])
         for g in range(PAIRS):
-            accumulate(0, 0, g, g, [1])
-        multiply(0, 0, 0)
-        quantize_weights(0, 1, slice(0, 1))
+            accumulate(REAL, HIGH, g, [0], PAIRS + g)
+        rows_of[REAL, 1] = after_rounding(REAL, HIGH, 0, [P, 2, H])
+        multiply(REAL, LOW, 1)
+        quantize_weights(REAL, HIGH, [1])
         for g in range(PAIRS):
-            accumulate(0, 1, g, 4 + g, [0])
-        parts[0, 1] = after_rounding(0, 1, 0, [P, 2, H])
-        multiply(0, 0, 1)
-        quantize_weights(0, 1, slice(1, 2))
-        for g in range(PAIRS):
-            accumulate(0, 1, g, 4 + g, [1])
-        held = after_rounding(0, 1, 1, [P, 2, 2, HALF])
-        for g in (2, 3):
-            parts[0, 0, g] = held[:, g - 2]
-            multiply(0, 0, g)
-        multiply(0, 1, 0)
-        multiply(0, 1, 1)
-        turn_part(0, 0, 0, 0)
-        turn_part(0, 0, 1, 1)
-        quantize_weights(1, 0, both)
-        held = after_rounding(1, 0, 1, [P, 2, 2, HALF])
-        for g in (2, 3):
-            parts[0, 1, g] = held[:, g - 2]
-            multiply(0, 1, g)
-        product(1, 0, 0, 2)
-        accumulate(1, 0, 1, 3, [0, 1])
-        turn_part(0, 1, 0, 4)
-        turn_part(0, 1, 1, 5)
+            accumulate(REAL, HIGH, g, [1])
+        two_halves = after_rounding(REAL, HIGH, 1, [P, 2, 2, HALF])
+        for place, g in enumerate(ADDED_ON_VECTOR):
+            halves_of[REAL, LOW, g] = two_halves[:, place]
+            multiply(REAL, LOW, g)
+        multiply(REAL, HIGH, 0)
+        multiply(REAL, HIGH, 1)
+        turn_product(REAL, 0, 0, 0)
+        turn_product(REAL, 0, 1, 1)
+
         for a in range(PASSES):
-            quantize_weights(1, 1, slice(a, a + 1))
-        parts[1, 1] = after_rounding(1, 1, 1, [P, 2, H])
-        multiply(1, 0, 1)
-        product(1, 1, 0, 6)
-        product(1, 1, 1, 7)
-        accumulate(1, 1, 2, 2, [0, 1])
-        for s in range(2):
-            turn_part(1, 0, s, None)
-            round_sum(nc.scalar.copy, 0, s)
-        multiply(1, 1, 2)
-        product(1, 0, 2, 3)
-        for s in range(2):
-            turn_part(1, 1, s, None)
-            round_sum(nc.scalar.copy, 1, s)
-        accumulate(1, 0, 3, 6, [0, 1])
-        add_parts(nc.vector, 2, both, 1)
+            quantize_weights(IMAG, LOW, [a])
+        halves_of[REAL, HIGH, 2] = after_rounding(IMAG, LOW, 1, [P, 2, HALF])[:]
+        multiply(REAL, HIGH, 2)
+        product(IMAG, LOW, 0, 2)
+        accumulate(IMAG, LOW, 1, [0, 1], 3)
+        turn_product(REAL, 1, 0, 4)
+        turn_product(REAL, 1, 1, 5)
+
+        for a in range(PASSES):
+            quantize_weights(IMAG, HIGH, [a])
+        rows_and_half = after_rounding(IMAG, HIGH, 1, [P, 3, H])
+        rows_of[IMAG, 1] = rows_and_half[:, :2]
+        halves_of[REAL, HIGH, 3] = rows_and_half[:, 2].rearrange("x (s c) -> x s c", s=2)
+        multiply(REAL, HIGH, 3)
+        product(IMAG, HIGH, 0, 6)
+        multiply(IMAG, LOW, 1)
+        product(IMAG, HIGH, 1, 7)
+        accumulate(IMAG, HIGH, 2, [0, 1], 2)
+        finish_sums(0)
+        multiply(IMAG, HIGH, 2)
+        product(IMAG, LOW, 2, 3)
+        finish_sums(1)
+        accumulate(IMAG, LOW, 3, [0, 1], 6)
+        add_halves(2, both, HIGH)
         beams(0, both, [0, 0, 1], [])
-        add_parts(nc.vector, 2, both, 0)
-        accumulate(1, 1, 3, 7, [0, 1])
-        multiply(1, 0, 3)
+        add_halves(2, both, LOW)
+        accumulate(IMAG, HIGH, 3, [0, 1], 7)
+        multiply(IMAG, LOW, 3)
         turn_words(nc.scalar.copy, 2, both, 2)
         beams(1, both, [4, 4, 5], [])
-        add_parts(nc.vector, 3, both, 0)
-        multiply(1, 1, 3)
-        for s in range(2):
-            add_parts(nc.vector, 3, slice(s, s + 1), 1)
-            turn_words((nc.scalar.copy, nc.vector.tensor_copy)[s], 3, slice(s, s + 1), (3, 6)[s])
+        add_halves(3, both, LOW)
+        multiply(IMAG, HIGH, 3)
+
+        first_tile, second_tile = slice(0, 1), slice(1, 2)
+        add_halves(3, first_tile, HIGH)
+        turn_words(nc.scalar.copy, 3, first_tile, 3)
+        add_halves(3, second_tile, HIGH)
+        turn_words(nc.vector.tensor_copy, 3, second_tile, 6)
         beams(2, both, [0, 1, 2], [1])
-        beams(3, slice(0, 1), [7, 4, 5], [1])
-        beams(3, slice(1, 2), [3, 6, 1], [1])
+        beams(3, first_tile, [7, 4, 5], [1])
+        beams(3, second_tile, [3, 6, 1], [1])

from contextlib import ExitStack

import concourse.mybir as mybir
from concourse.masks import make_identity

K, K2, H, N, T, T2, S = 1024, 512, 512, 384, 4096, 2048, 1024
FLOPS = 2 * S * (2 * K * H + 2 * K2 * H + H * N)

F32 = mybir.dt.float32
BF16 = mybir.dt.bfloat16
I32 = mybir.dt.int32
U32 = mybir.dt.uint32
U16 = mybir.dt.uint16
U8 = mybir.dt.uint8
FP8X4 = mybir.dt.float8_e4m3fn_x4
FP4X4 = mybir.dt.float4_e2m1fn_x4
MULT = mybir.AluOpType.mult
ADD = mybir.AluOpType.add
IDENTITY = mybir.ActivationFunctionType.Identity

P = 128
PACK = 4
K_PASS = P * PACK
PASSES = K // K_PASS
TOK = 128
TILES = S // TOK
PAIR = 2 * TOK
PAIRS = S // PAIR
HALF = H // 2
BEAM_TILES = N // P
SCALE_ROW = (4, 8)
REAL, IMAG = 0, 1
LOW, HIGH = 0, 1
PIECES = ((REAL, LOW), (REAL, HIGH), (IMAG, LOW), (IMAG, HIGH))
SUMMED_IN_PSUM = (0, 1)
ADDED_ON_VECTOR = (2, 3)
REFERENCE_BANKS = (5, 6, 7)


def tile_list_reference_matched_beams_kernel(
    tc, tab_words, tab_scales, tab2_words, tab2_scales, offs, offs2, war, wai,
    wbr_words, wbr_scales, wbi_words, wbi_scales, beam_words, beam_scales, gain, base, out,
):
    nc = tc.nc
    with ExitStack() as ctx:
        lists = ctx.enter_context(tc.tile_pool(name="lists", bufs=1))
        keep = ctx.enter_context(tc.tile_pool(name="keep", bufs=1))
        psum = ctx.enter_context(tc.psum_pool(name="psum", bufs=1))

        def sbuf(name, shape, dtype):
            return keep.tile(shape, dtype, name=name, align_bytes=64)

        idx = lists.tile([P, S // 16], U16, name="idx")
        idx2 = lists.tile([P, S // 16], U16, name="idx2")

        v_words = [sbuf(f"v_words{a}", [P, T], I32) for a in range(PASSES)]
        v_scales = sbuf("v_scales", [P, T // 4], I32)
        v2_words = sbuf("v2_words", [P, T2], I32)
        v2_scales = sbuf("v2_scales", [P, T2 // 4], I32)
        wb_words = [sbuf(f"wb_words{m}", [P, 2 * H // 4], I32) for m in (REAL, IMAG)]
        wb_scales = [sbuf(f"wb_scales{m}", [P, H // 4], I32) for m in (REAL, IMAG)]
        bm_words = sbuf("bm_words", [P, N], I32)
        bm_scales = sbuf("bm_scales", [P, N // 4], I32)
        gain_cols = sbuf("gain_cols", [P, BEAM_TILES], F32)
        base_cols = sbuf("base_cols", [P, BEAM_TILES], F32)
        ident = sbuf("ident", [P, P], F32)

        nc.gpsimd.memset(v2_scales[:], 0)
        nc.vector.memset(v_scales[:], 0)
        nc.vector.memset(wb_scales[REAL][:], 0)
        nc.vector.memset(wb_scales[IMAG][:], 0)
        nc.vector.memset(bm_scales[:], 0)

        def load_scale_rows(scale_tile, rows):
            for r in range(4):
                nc.sync.dma_start(out=scale_tile[r:P:32, :], in_=rows[0, r:16:4, :].bitcast(I32))

        def words_of(dram, a):
            return dram[a].rearrange("p t i -> p (t i)").bitcast(I32)

        def load_table(a, first, last):
            cols = slice(first, last)
            nc.sync.dma_start(out=v_words[a][:, cols], in_=words_of(tab_words, a)[:, cols])

        nc.sync.dma_start(idx2[:], offs2)
        nc.sync.dma_start(out=wb_words[REAL][:], in_=wbr_words[0].bitcast(I32))
        nc.sync.dma_start(out=v2_words[:, : T2 // 2], in_=words_of(tab2_words, 0)[:, : T2 // 2])
        load_scale_rows(v2_scales, tab2_scales)
        nc.sync.dma_start(out=v2_words[:, T2 // 2 :], in_=words_of(tab2_words, 0)[:, T2 // 2 :])
        load_table(0, 0, T // 4)
        load_scale_rows(wb_scales[REAL], wbr_scales)
        for quadrant in range(4):
            nc.gpsimd.dma_start(
                out=v_scales[32 * quadrant + SCALE_ROW[0] : 32 * quadrant + SCALE_ROW[1] + 4, :],
                in_=tab_scales[:, 4 * quadrant : 4 * quadrant + 4, :].bitcast(I32),
            )
        nc.sync.dma_start(idx[:], offs)
        load_table(0, T // 4, T)
        nc.sync.dma_start(out=wb_words[IMAG][:], in_=wbi_words[0].bitcast(I32))
        load_scale_rows(wb_scales[IMAG], wbi_scales)

        wa_raw = {}
        for m, half in PIECES:
            if (m, half) == PIECES[1]:
                load_table(1, 0, T // 2)
                load_table(1, T // 2, T)
            for a in range(PASSES):
                raw = sbuf(f"wa_raw{m}{half}{a}", [P, PACK, HALF], F32)
                rows = (war, wai)[m][a * K_PASS : (a + 1) * K_PASS, half * HALF : (half + 1) * HALF]
                nc.sync.dma_start(out=raw[:], in_=rows.rearrange("(p j) c -> p j c", j=PACK))
                wa_raw[m, half, a] = raw
        nc.sync.dma_start(out=bm_words[:], in_=words_of(beam_words, 0))
        load_scale_rows(bm_scales, beam_scales)
        with nc.allow_non_contiguous_dma(reason="one gain and one baseline for each partition"):
            nc.sync.dma_start(out=gain_cols[:], in_=gain.rearrange("(c p) -> p c", p=P))
            nc.sync.dma_start(out=base_cols[:], in_=base.rearrange("(c p) -> p c", p=P))
        make_identity(nc, ident[:])

        def gather(picked, window, offsets, first, last):
            nc.vector.tensor_copy(picked[:, first:last], window.indirect(offsets[:, first // 16 : last // 16]))

        g_words = [sbuf(f"g_words{a}", [P, S], U32) for a in range(PASSES)]
        g_scales = sbuf("g_scales", [P, S], U8)
        g2_words = sbuf("g2_words", [P, S], U32)
        g2_scales = sbuf("g2_scales", [P, S], U8)

        gather(g2_scales, v2_scales[:].bitcast(U8), idx2, 0, S)
        for first, last in ((0, PAIR), (PAIR, 2 * PAIR), (2 * PAIR, S)):
            gather(g2_words, v2_words[:].bitcast(U32), idx2, first, last)
        gather(g_words[0], v_words[0][:].bitcast(U32), idx, 0, S)
        gather(g_scales, v_scales[:].bitcast(U8), idx, 0, S)

        def bank(n, shape):
            return psum.tile(shape, F32, name=f"bank{n}", tag=f"bank{n}", bufs=1)

        b_vals = sbuf("b_vals", [P, 2, TILES, H], F32)

        def reference_channels(m):
            for j in range(TILES):
                tok = slice(j * TOK, (j + 1) * TOK)
                acc = bank(REFERENCE_BANKS[(m * TILES + j) % len(REFERENCE_BANKS)], [P, H])
                nc.tensor.matmul_mx(
                    out=acc[:],
                    lhsT=g2_words[:, tok].bitcast(FP8X4),
                    lhsT_scale=g2_scales[:, tok],
                    rhs=wb_words[m][:].bitcast(U8).bitcast(FP4X4),
                    rhs_scale=wb_scales[m][:].bitcast(U8),
                    start=True,
                    stop=True,
                )
                if j // 2 in SUMMED_IN_PSUM:
                    nc.scalar.copy(
                        out=b_vals[:, m, j, :].rearrange("x (t p) -> x t p", t=PACK),
                        in_=acc[:].rearrange("x (p t) -> x t p", t=PACK),
                    )
                else:
                    nc.scalar.copy(
                        out=b_vals[:, m, j, :].rearrange("x (u p e) -> x u p e", u=2, e=2),
                        in_=acc[:].rearrange("x (p u e) -> x u p e", u=2, e=2),
                    )

        wa_bf = {(m, half): sbuf(f"wa_bf{m}{half}", [P, PASSES, HALF, PACK], BF16) for m, half in PIECES}

        def round_weights(copy, m, half, a):
            copy(
                out=wa_bf[m, half][:, a, :, :].rearrange("x (u q e) j -> x q j u e", u=2, e=2),
                in_=wa_raw[m, half, a][:].rearrange("x j (q u e) -> x q j u e", u=2, e=2),
            )

        weights = {
            (m, half): (
                sbuf(f"wa_codes{m}{half}", [P, PASSES, HALF], U32),
                sbuf(f"wa_scales{m}{half}", [P, PASSES, HALF], U8),
            )
            for m, half in PIECES
        }

        def quantize_weights(m, half, passes):
            codes, scales = weights[m, half]
            span = slice(passes[0], passes[-1] + 1)
            nc.vector.quantize_mx(
                out=codes[:, span, :].rearrange("x a c -> x (a c)").bitcast(FP8X4),
                scales=scales[:, span, :].rearrange("x a c -> x (a c)"),
                in_=wa_bf[m, half][:, span].rearrange("x a c j -> x (a c j)"),
            )

        def after_rounding(m, half, a, shape):
            return keep.tile(shape, F32, name=f"after{m}{half}{a}", tag=f"wa_raw{m}{half}{a}", align_bytes=64)

        rows_of = {(m, 0): sbuf(f"rows_of{m}0", [P, 2, H], F32) for m in (REAL, IMAG)}
        halves_of = {}
        for half in (LOW, HIGH):
            for g in ADDED_ON_VECTOR:
                halves_of[IMAG, half, g] = sbuf(f"halves_of1{half}{g}", [P, 2, HALF], F32)[:]

        accs = {}

        def accumulate(m, half, g, passes, n=None):
            codes, scales = weights[m, half]
            if 0 in passes:
                accs[m, half, g] = bank(n, [P, 2, HALF])
            for a in passes:
                for s in range(2):
                    tok = slice(g * PAIR + s * TOK, g * PAIR + (s + 1) * TOK)
                    nc.tensor.matmul_mx(
                        out=accs[m, half, g][:, s, :],
                        lhsT=g_words[a][:, tok].bitcast(FP8X4),
                        lhsT_scale=g_scales[SCALE_ROW[a] :, tok],
                        rhs=codes[:, a, :].bitcast(FP8X4),
                        rhs_scale=scales[:, a, :],
                        start=(a == 0 and s == 0),
                        stop=(a == PASSES - 1 and s == 1),
                    )

        def multiply(m, half, g):
            acc = accs[m, half, g]
            refs = b_vals[:, m, 2 * g : 2 * g + 2, :]
            if g in SUMMED_IN_PSUM:
                view = "x s (u e h q) -> x (s u) e h q"
                nc.vector.tensor_tensor(
                    rows_of[m, g][:].rearrange(view, u=2, e=2, h=2)[:, :, :, half, :],
                    acc[:].rearrange("x s (u q e) -> x (s u) e q", u=2, e=2),
                    refs.rearrange(view, u=2, e=2, h=2)[:, :, :, half, :],
                    MULT,
                )
            else:
                nc.vector.tensor_tensor(
                    halves_of[m, half, g].rearrange("x s (u c) -> x (s u) c", u=2),
                    acc[:].rearrange("x s (u c) -> x (s u) c", u=2),
                    refs.rearrange("x s (u h c) -> x (s u) h c", u=2, h=2)[:, :, half, :],
                    MULT,
                )

        def product(m, half, g, n):
            accumulate(m, half, g, [0, 1], n)
            multiply(m, half, g)

        sums = {}

        def turn_product(m, g, s, n=None):
            if m == REAL:
                sums[g, s] = bank(n, [P, PACK, TOK])
            for t in range(PACK):
                nc.tensor.matmul(
                    sums[g, s][:, t, :], rows_of[m, g][:, s, t * P : (t + 1) * P], ident[:],
                    start=(m == REAL and t == 0), stop=(m == IMAG and t == PACK - 1), is_transpose=True,
                )

        h_bf = [sbuf(f"h_bf{g}", [P, 2, TOK * PACK], BF16) for g in range(PAIRS)]

        def finish_sums(g):
            for s in range(2):
                turn_product(IMAG, g, s)
                nc.scalar.copy(
                    out=h_bf[g][:, s, :].rearrange("p (j t) -> p j t", t=PACK),
                    in_=sums[g, s][:].rearrange("p t j -> p j t"),
                )

        h_tok = {g: sbuf(f"h_tok{g}", [P, 2, H], BF16) for g in ADDED_ON_VECTOR}

        def add_halves(g, tiles, half):
            nc.vector.tensor_tensor(
                h_tok[g][:, tiles, :].rearrange("x s (u h c) -> x s u h c", u=2, h=2)[:, :, :, half, :],
                halves_of[REAL, half, g][:, tiles, :].rearrange("x s (u c) -> x s u c", u=2),
                halves_of[IMAG, half, g][:, tiles, :].rearrange("x s (u c) -> x s u c", u=2),
                ADD,
            )

        def turn_words(copy, g, tiles, n):
            count = tiles.stop - tiles.start
            turned = bank(n, [P, count, 2, TOK])
            for s in range(count):
                words = h_tok[g][:, tiles.start + s, :].bitcast(F32)
                for u in range(2):
                    nc.tensor.transpose(turned[:, s, u, :], words[:, u * P : (u + 1) * P], ident[:])
            copy(
                out=h_bf[g][:, tiles, :].bitcast(F32).rearrange("p s (j u) -> p s j u", u=2),
                in_=turned[:].rearrange("p s u j -> p s j u"),
            )

        results = [sbuf(f"result{g}", [P, BEAM_TILES, PAIR], F32) for g in range(PAIRS)]

        def beams(g, tiles, banks, on_vector):
            width = (tiles.stop - tiles.start) * TOK
            first = g * PAIR + tiles.start * TOK
            codes = sbuf(f"h_codes{first}", [P, width], U32)
            scales = sbuf(f"h_scales{first}", [P, width], U8)
            nc.vector.quantize_mx(
                out=codes[:].bitcast(FP8X4), scales=scales[:],
                in_=h_bf[g][:, tiles, :].rearrange("p s c -> p (s c)"),
            )
            result = results[g][:, :, tiles.start * TOK : tiles.stop * TOK]
            rows = out[:, g * PAIR : (g + 1) * PAIR].rearrange("(c p) j -> p c j", p=P)
            in_bank = {n: bank(n, [P, banks.count(n), width]) for n in sorted(set(banks))}
            ys = [in_bank[n][:, banks[:c].count(n), :] for c, n in enumerate(banks)]
            for c in range(BEAM_TILES):
                cols = slice(c * P, (c + 1) * P)
                nc.tensor.matmul_mx(
                    out=ys[c],
                    lhsT=bm_words[:, cols].bitcast(FP8X4),
                    lhsT_scale=bm_scales[:].bitcast(U8)[:, cols],
                    rhs=codes[:].bitcast(FP8X4),
                    rhs_scale=scales[:],
                    start=True,
                    stop=True,
                )
            stored_by_tile = g >= PAIRS - 2
            for c in range(BEAM_TILES):
                if c in on_vector:
                    nc.vector.tensor_scalar(
                        out=result[:, c, :], in0=ys[c], scalar1=gain_cols[:, c : c + 1],
                        scalar2=base_cols[:, c : c + 1], op0=MULT, op1=ADD,
                    )
                else:
                    nc.scalar.activation(
                        out=result[:, c, :], in_=ys[c], func=IDENTITY,
                        bias=base_cols[:, c : c + 1], scale=gain_cols[:, c : c + 1],
                    )
                if stored_by_tile and tiles.stop == 2:
                    queue = nc.scalar if (g, c) == (PAIRS - 1, BEAM_TILES - 1) else nc.sync
                    queue.dma_start(out=rows[:, c, :], in_=results[g][:, c, :])
            if not stored_by_tile:
                nc.sync.dma_start(out=rows, in_=result[:])

        reference_channels(REAL)
        reference_channels(IMAG)
        for a in range(PASSES):
            round_weights(nc.vector.tensor_copy, REAL, LOW, a)
        for m, half in PIECES[1:]:
            for a in range(PASSES):
                round_weights(nc.scalar.copy, m, half, a)

        both = slice(0, 2)

        quantize_weights(REAL, LOW, [0, 1])
        for g in range(PAIRS):
            accumulate(REAL, LOW, g, [0], g)
        for first in (0, S // 2):
            gather(g_words[1], v_words[1][:].bitcast(U32), idx, first, first + S // 2)
        for g in range(PAIRS):
            accumulate(REAL, LOW, g, [1])

        multiply(REAL, LOW, 0)
        quantize_weights(REAL, HIGH, [0])
        for g in range(PAIRS):
            accumulate(REAL, HIGH, g, [0], PAIRS + g)
        rows_of[REAL, 1] = after_rounding(REAL, HIGH, 0, [P, 2, H])
        multiply(REAL, LOW, 1)
        quantize_weights(REAL, HIGH, [1])
        for g in range(PAIRS):
            accumulate(REAL, HIGH, g, [1])
        two_halves = after_rounding(REAL, HIGH, 1, [P, 2, 2, HALF])
        for place, g in enumerate(ADDED_ON_VECTOR):
            halves_of[REAL, LOW, g] = two_halves[:, place]
            multiply(REAL, LOW, g)
        multiply(REAL, HIGH, 0)
        multiply(REAL, HIGH, 1)
        turn_product(REAL, 0, 0, 0)
        turn_product(REAL, 0, 1, 1)

        for a in range(PASSES):
            quantize_weights(IMAG, LOW, [a])
        halves_of[REAL, HIGH, 2] = after_rounding(IMAG, LOW, 1, [P, 2, HALF])[:]
        multiply(REAL, HIGH, 2)
        product(IMAG, LOW, 0, 2)
        accumulate(IMAG, LOW, 1, [0, 1], 3)
        turn_product(REAL, 1, 0, 4)
        turn_product(REAL, 1, 1, 5)

        for a in range(PASSES):
            quantize_weights(IMAG, HIGH, [a])
        rows_and_half = after_rounding(IMAG, HIGH, 1, [P, 3, H])
        rows_of[IMAG, 1] = rows_and_half[:, :2]
        halves_of[REAL, HIGH, 3] = rows_and_half[:, 2].rearrange("x (s c) -> x s c", s=2)
        multiply(REAL, HIGH, 3)
        product(IMAG, HIGH, 0, 6)
        multiply(IMAG, LOW, 1)
        product(IMAG, HIGH, 1, 7)
        accumulate(IMAG, HIGH, 2, [0, 1], 2)
        finish_sums(0)
        multiply(IMAG, HIGH, 2)
        product(IMAG, LOW, 2, 3)
        finish_sums(1)
        accumulate(IMAG, LOW, 3, [0, 1], 6)
        add_halves(2, both, HIGH)
        beams(0, both, [0, 0, 1], [])
        add_halves(2, both, LOW)
        accumulate(IMAG, HIGH, 3, [0, 1], 7)
        multiply(IMAG, LOW, 3)
        turn_words(nc.scalar.copy, 2, both, 2)
        beams(1, both, [4, 4, 5], [])
        add_halves(3, both, LOW)
        multiply(IMAG, HIGH, 3)

        first_tile, second_tile = slice(0, 1), slice(1, 2)
        add_halves(3, first_tile, HIGH)
        turn_words(nc.scalar.copy, 3, first_tile, 3)
        add_halves(3, second_tile, HIGH)
        turn_words(nc.vector.tensor_copy, 3, second_tile, 6)
        beams(2, both, [0, 1, 2], [1])
        beams(3, first_tile, [7, 4, 5], [1])
        beams(3, second_tile, [3, 6, 1], [1])
